import numpy as np
import ml_dtypes


def mxq(x, axis, fmt="e4m3"):
    dtype, down = {"e4m3": (ml_dtypes.float8_e4m3fn, 7), "e5m2": (ml_dtypes.float8_e5m2, 14)}[fmt]
    v = np.moveaxis(np.asarray(x, np.float32).astype(ml_dtypes.bfloat16).astype(np.float64), axis, -1)
    blocks = v.reshape(v.shape[:-1] + (-1, 32))
    amax = np.abs(blocks).max(-1, keepdims=True)
    byte = np.maximum(np.where(amax > 0, np.frexp(amax)[1] - 1 + 127, 0) - down, 1)
    scale = np.exp2(byte - 127.0)
    codes = (blocks / scale).astype(np.float32).astype(dtype).astype(np.float64)
    return np.moveaxis((codes * scale).reshape(v.shape), -1, axis)


WIDE = False


def mx_kscale(k):
    if not WIDE:
        return np.ones(k)
    levels = np.array([10, -10, 5, -5, 0])
    if k % 512:
        return np.exp2(np.random.permutation(np.resize(levels, k // 32))).repeat(32)
    a = np.empty((k // 512, 16))
    for p in range(k // 512):
        a[p, :8] = np.random.permutation(np.resize(levels, 8))
        for g in range(8):
            far = levels[np.abs(levels - a[p, g]) >= 10]
            a[p, g + 8] = far[np.random.randint(len(far))]
    return np.exp2(a.ravel()).repeat(32)


def f64(x):
    return np.asarray(x).astype(np.float64)


def striped(idx):
    return np.tile(idx.reshape(-1, 16).T, (8, 1)).astype(np.uint16)


def unstriped(offs):
    return offs[:16].T.reshape(-1).astype(np.int64)


E2M1 = np.array([0.0, 0.5, 1.0, 1.5, 2.0, 3.0, 4.0, 6.0, -0.0, -0.5, -1.0, -1.5, -2.0, -3.0, -4.0, -6.0])


def pack_weight(w, fmt):
    k, n = w.shape
    w = f64(np.asarray(w, np.float32).astype(ml_dtypes.bfloat16)).reshape(k // 32, 32, n)
    amax = np.abs(w).max(1)
    if fmt == "e4m3":
        byte = np.frexp(amax)[1] - 1 + 127 - 7
    else:
        mant, ex = np.frexp(amax / 6.0)
        byte = np.where(mant > 0.5, ex, ex - 1) + 127
    byte = np.clip(np.where(amax > 0, byte, 1), 1, 254)
    scaled = (w * np.exp2(127.0 - byte)[:, None, :]).reshape(k, n).astype(np.float32)
    by_word = np.ascontiguousarray(scaled.reshape(k // 512, 128, 4, n).transpose(0, 1, 3, 2))
    if fmt == "e4m3":
        words = by_word.astype(ml_dtypes.float8_e4m3fn).view(np.uint8)
    else:
        c = by_word.astype(ml_dtypes.float4_e2m1fn).view(np.uint8) & 0xF
        words = (c[..., 0::2] | (c[..., 1::2] << 4)).reshape(k // 512, 128, 2 * n)
    return np.ascontiguousarray(words), np.ascontiguousarray(byte.astype(np.uint8).reshape(k // 512, 16, n))


def unpack_weight(words, scales, fmt):
    g, _, n = scales.shape
    words = np.ascontiguousarray(words).reshape(g, 128, n, -1)
    if fmt == "e4m3":
        vals = words.view(ml_dtypes.float8_e4m3fn).astype(np.float64)
    else:
        nib = np.empty((g, 128, n, 4), np.uint8)
        nib[..., 0::2] = words & 0xF
        nib[..., 1::2] = words >> 4
        vals = E2M1[nib]
    vals = vals * np.repeat(np.exp2(scales.astype(np.float64) - 127.0), 8, axis=1)[..., None]
    return vals.transpose(0, 1, 3, 2).reshape(g * 512, n)


def relu(v):
    return np.maximum(v, 0.0)


K, T, E1, C1, E2, C2, H = 1024, 768, 6, 256, 6, 256, 512
N = 256


def deal(E, C):
    first = np.random.permutation(np.repeat(np.arange(E), T // E))
    second = (first + 1 + np.random.permutation(np.repeat(np.arange(E - 1), -(-T // (E - 1)))[:T])) % E
    while np.bincount(second, minlength=E).max() != T // E:
        load = np.bincount(second, minlength=E); hi, lo = int(load.argmax()), int(load.argmin())
        t = np.flatnonzero((second == hi) & (first != lo))[0]; second[t] = lo
    slot_token = np.empty(E * C, np.int64); pos = np.empty((2, T), np.int64); fill = np.zeros(E, np.int64)
    place = np.stack([np.random.permutation(C) for _ in range(E)])
    for r, deal in enumerate((first, second)):
        for t in np.random.permutation(T):
            e = deal[t]; j = e * C + place[e, fill[e]]; fill[e] += 1; slot_token[j] = t; pos[r, t] = j
    g = np.random.uniform(0.2, 0.8, T)
    return slot_token, pos, np.stack([g, 1.0 - g])


def by_expert(wq, xq, E, C):
    return np.concatenate([wq[e].T @ xq[:, e * C:(e + 1) * C] for e in range(E)], axis=1)


def setup_inputs():
    n = np.random.standard_normal
    s = mx_kscale(K)
    u = mx_kscale(H)
    slots1, pos1, g1 = deal(E1, C1)
    slots2, pos2, g2 = deal(E2, C2)
    x = pack_weight(n((K, T)) * s[:, None], "e4m3")
    w1 = [pack_weight(m, "e4m3") for m in n((E1, K, H)) / np.sqrt(K) / s[None, :, None] * u]
    w2 = [pack_weight(m, "e4m3") for m in n((E2, H, N)) / np.sqrt(H) / u[None, :, None]]
    return {
        "x_words": x[0],
        "x_scales": x[1],
        "w1_words": np.stack([m[0] for m in w1]),
        "w1_scales": np.stack([m[1] for m in w1]),
        "w2_words": np.stack([m[0] for m in w2]),
        "w2_scales": np.stack([m[1] for m in w2]),
        "gate1": (np.stack([np.tile(r, (128, 1)) for r in g1])).astype(np.float32),
        "gate2": (np.stack([np.tile(r, (128, 1)) for r in g2])).astype(np.float32),
        "offs": striped(slots1),
        "pos1": striped(pos1[0]),
        "pos2": striped(pos1[1]),
        "offs2": striped(slots2),
        "pos3": striped(pos2[0]),
        "pos4": striped(pos2[1]),
    }


def reference(x_words, x_scales, w1_words, w1_scales, w2_words, w2_scales, gate1, gate2, offs, pos1, pos2, offs2, pos3, pos4):
    w1 = np.stack([unpack_weight(w1_words[e], w1_scales[e], "e4m3") for e in range(E1)])
    w2 = np.stack([unpack_weight(w2_words[e], w2_scales[e], "e4m3") for e in range(E2)])
    idx, idx2 = unstriped(offs), unstriped(offs2)
    xq = unpack_weight(x_words, x_scales, "e4m3")[:, idx]
    h = relu(by_expert(w1, xq, E1, C1))
    c = sum(f64(gate1[r, :1]) * h[:, unstriped(p)] for r, p in enumerate((pos1, pos2)))
    y = by_expert(w2, mxq(c[:, idx2], 0, "e4m3"), E2, C2)
    out = sum(f64(gate2[r, :1]) * y[:, unstriped(p)] for r, p in enumerate((pos3, pos4)))
    return out

@@ -1,0 +1,237 @@
+from contextlib import ExitStack
+
+import concourse.mybir as mybir
+from concourse.masks import make_identity
+
+K, T, E, C, H, N = 1024, 768, 6, 256, 512, 256
+S = E * C
+P = 128
+FLOPS = 2 * S * (K * H + H * N)
+
+F32 = mybir.dt.float32
+BF16 = mybir.dt.bfloat16
+I32 = mybir.dt.int32
+U32 = mybir.dt.uint32
+U16 = mybir.dt.uint16
+U8 = mybir.dt.uint8
+FP8X4 = mybir.dt.float8_e4m3fn_x4
+MULT = mybir.AluOpType.mult
+RELU = mybir.ActivationFunctionType.Relu
+
+X_PLANE = 8
+EXPERT_RUNS_1 = ((0,), (1,), (2, 3), (4,), (5,))
+TOKEN_RUNS_1 = ((0, 1, 2), (3, 4), (5,))
+OUT_RUNS = ((0, 0, 768), (1, 0, 512), (1, 512, 768))
+
+
+def entries(lst, first, last):
+    return lst[:, first // 16 : last // 16]
+
+
+def tile_moe_ser_relu_kernel(
+    tc, x_words, x_scales, w1_words, w1_scales, w2_words, w2_scales, gate1, gate2,
+    offs, pos1, pos2, offs2, pos3, pos4, out,
+):
+    nc = tc.nc
+    with ExitStack() as ctx:
+        sb = ctx.enter_context(tc.tile_pool(name="sb", bufs=1))
+        ps = ctx.enter_context(tc.psum_pool(name="ps", bufs=1))
+        banks = [ps.tile([P, 512], F32, name=f"bank{b}") for b in range(8)]
+
+        def load_list(src, name):
+            lst = sb.tile(list(src.shape), U16, name=name)
+            nc.sync.dma_start(lst[:], src)
+            return lst
+
+        xs = sb.tile([P, T], U8, name="xs", align_bytes=64)
+        w1s = sb.tile([P, E // 2, H], U8, name="w1s", align_bytes=64)
+        w2s = sb.tile([P, E, N], U8, name="w2s", align_bytes=64)
+        nc.gpsimd.memset(xs[:].bitcast(I32), 0)
+        xs_in = sb.tile([P, T], U8, name="xs_in", align_bytes=64)
+        for q in range(4):
+            nc.gpsimd.memset(xs_in[32 * q : 32 * q + X_PLANE, :].bitcast(I32), 0)
+        nc.vector.memset(w2s[:].bitcast(I32), 0)
+        ident = sb.tile([P, P], F32, name="ident", align_bytes=64)
+        make_identity(nc, ident[:])
+
+        offs_t = load_list(offs, "offs_t")
+        xw = [sb.tile([P, T], U32, name=f"xw{s}", align_bytes=64) for s in range(2)]
+        x_passes = x_words.rearrange("s p t d -> s p (t d)")
+        nc.scalar.dma_start(xw[0][:].bitcast(I32), x_passes[0].bitcast(I32))
+        for q in range(4):
+            nc.sync.dma_start(
+                xs_in[32 * q + X_PLANE : 32 * q + X_PLANE + 8, :].bitcast(I32),
+                x_scales[:, 4 * q : 4 * q + 4, :].bitcast(I32),
+            )
+            rows = slice(32 * q, 32 * q + X_PLANE + 8)
+            nc.vector.tensor_copy(xs[rows, :].bitcast(I32), xs_in[rows, :].bitcast(I32))
+        nc.sync.dma_start(xw[1][:].bitcast(I32), x_passes[1].bitcast(I32))
+        w1w = [sb.tile([P, 4, H], U32, name=f"w1w{g}", align_bytes=64) for g in range(E // 2)]
+        w1_passes = w1_words.rearrange("e s p i d -> p (e s) (i d)")
+        w1_rows = w1_scales.rearrange("e s b i -> (e s) b i")
+
+        def load_w1_words(first, last):
+            g, a = first // 2, 2 * (first % 2)
+            nc.sync.dma_start(
+                w1w[g][:, a : a + 2 * (last - first), :].bitcast(I32),
+                w1_passes[:, 2 * first : 2 * last, :].bitcast(I32),
+            )
+
+        def load_w1_scales(g):
+            if g < E // 2 - 1:
+                spans = [(32 * q, 4 * g, 8, q) for q in range(4)]
+            else:
+                spans = [(0, 4 * g, 4, 0)] + [(32 * q - 16, 4 * g - 4, 8, q) for q in range(1, 4)] + [(P - 16, 4 * g, 4, 3)]
+            for first, pass0, count, q in spans:
+                nc.sync.dma_start(
+                    w1s[first : first + 4 * count, g, :].bitcast(I32),
+                    w1_rows[pass0 : pass0 + count, 4 * q : 4 * q + 4, :].bitcast(I32),
+                )
+
+        load_w1_words(0, 1)
+        load_w1_scales(0)
+        load_w1_words(1, 2)
+        for g in range(1, E // 2):
+            load_w1_scales(g)
+            load_w1_words(2 * g, 2 * g + 2)
+        pos_1 = [load_list(pos1, "pos1_t"), load_list(pos2, "pos2_t")]
+        g1 = sb.tile([P, 2, T], F32, name="g1")
+        nc.sync.dma_start(g1[:], gate1.rearrange("r p t -> p r t"))
+        offs2_t = load_list(offs2, "offs2_t")
+        w2w = sb.tile([P, E, N], U32, name="w2w", align_bytes=64)
+        nc.sync.dma_start(w2w[:].bitcast(I32), w2_words.rearrange("e s p n d -> p (e s) (n d)").bitcast(I32))
+        w2_rows = w2_scales.rearrange("e s (q r) n -> r q (e s) n", r=4)
+        for r in range(4):
+            nc.sync.dma_start(w2s[r:P:32, :, :].bitcast(I32), w2_rows[r].bitcast(I32))
+        pos_2 = [load_list(pos3, "pos3_t"), load_list(pos4, "pos4_t")]
+        g2 = sb.tile([P, 2, T], F32, name="g2")
+        nc.sync.dma_start(g2[:], gate2.rearrange("r p t -> p r t"))
+
+        xg = [sb.tile([P, S], U32, name=f"xg{s}", align_bytes=64) for s in range(2)]
+        xgs = sb.tile([P, S], U8, name="xgs", align_bytes=64)
+        h = [sb.tile([P, S], F32, name=f"h{j}", align_bytes=64) for j in range(4)]
+        for run, experts in enumerate(EXPERT_RUNS_1):
+            lo, hi = experts[0] * C, (experts[-1] + 1) * C
+            picked = entries(offs_t, lo, hi)
+            nc.vector.tensor_copy(xg[0][:, lo:hi], xw[0][:].indirect(picked))
+            nc.vector.tensor_copy(xgs[:, lo:hi], xs[:].indirect(picked))
+            nc.vector.tensor_copy(xg[1][:, lo:hi], xw[1][:].indirect(picked))
+            acc = banks[4 * (run % 2) : 4 * (run % 2) + 4]
+
+            def one_pass(e, s, j):
+                a = 2 * (e % 2) + s
+                slots = slice(e * C, (e + 1) * C)
+                cols = slice(j * P, (j + 1) * P)
+                nc.tensor.matmul_mx(
+                    acc[j][:, e * C - lo : (e + 1) * C - lo],
+                    lhsT=w1w[e // 2][:, a, cols].bitcast(FP8X4),
+                    lhsT_scale=w1s[4 * a : P, e // 2, cols],
+                    rhs=xg[s][:, slots].bitcast(FP8X4),
+                    rhs_scale=xgs[X_PLANE + 4 * s : P, slots],
+                    start=(s == 0),
+                    stop=(s == 1),
+                )
+
+            if len(experts) == 1:
+                for j in range(4):
+                    one_pass(experts[0], 0, j)
+            for j in range(4):
+                for e in experts:
+                    if len(experts) > 1:
+                        one_pass(e, 0, j)
+                    one_pass(e, 1, j)
+                nc.scalar.activation(h[j][:, lo:hi], acc[j][:, : hi - lo], RELU)
+
+        prod = [[sb.tile([P, T], F32, name=f"prod{j}_{r}", align_bytes=64) for r in range(2)] for j in range(4)]
+        c_rows = [sb.tile([P, 2, P, 2], BF16, name=f"c_rows{t}", align_bytes=64) for t in range(T // P)]
+        c_pairs = sb.tile([P, 2, T], U32, name="c_pairs", align_bytes=64)
+        last_tile = T // P - 1
+        for tiles in TOKEN_RUNS_1:
+            lo, hi = tiles[0] * P, (tiles[-1] + 1) * P
+            for j in range(4):
+                for r in range(2):
+                    nc.vector.tensor_tensor(
+                        prod[j][r][:, lo:hi], h[j][:].indirect(entries(pos_1[r], lo, hi)), g1[:, r, lo:hi], MULT
+                    )
+                for t in tiles:
+                    bank = banks[0] if (t == last_tile and j == 3) else banks[t]
+                    for r in range(2):
+                        nc.tensor.matmul(
+                            bank[:, j * P : (j + 1) * P],
+                            lhsT=prod[j][r][:, t * P : (t + 1) * P],
+                            rhs=ident[:],
+                            is_transpose=True,
+                            start=(r == 0),
+                            stop=(r == 1),
+                        )
+                    if t == last_tile and j >= 2:
+                        p0, p1 = (0, 96) if j == 2 else (96, 128)
+                        nc.scalar.copy(
+                            c_rows[t][:, :, p0:p1, :],
+                            bank[:, 4 * p0 : 4 * p1].rearrange("t (p u e) -> t u p e", u=2, e=2),
+                        )
+            for t in tiles:
+                if t != last_tile:
+                    nc.scalar.copy(c_rows[t][:], banks[t][:].rearrange("t (p u e) -> t u p e", u=2, e=2))
+                back = banks[6 + t % 2]
+                for u in range(2):
+                    nc.tensor.transpose(
+                        back[:, u * P : (u + 1) * P],
+                        c_rows[t][:, u].rearrange("t p e -> t (p e)").bitcast(F32),
+                        ident[:],
+                    )
+                nc.scalar.copy(
+                    c_pairs[:, :, t * P : (t + 1) * P].bitcast(BF16),
+                    back[:, : 2 * P].bitcast(BF16).rearrange("p (u t) -> p u t", u=2),
+                )
+
+        cg = sb.tile([P, S, 2], U32, name="cg", align_bytes=64)
+        cq = sb.tile([P, S], U32, name="cq", align_bytes=64)
+        cqs = sb.tile([P, S], U8, name="cqs", align_bytes=64)
+        y = [sb.tile([P, S], F32, name=f"y{n}", align_bytes=64) for n in range(2)]
+
+        def gather_c(f, u):
+            lo, hi = f * C, (f + 1) * C
+            nc.vector.tensor_copy(cg[:, lo:hi, u], c_pairs[:, u, :].indirect(entries(offs2_t, lo, hi)))
+
+        def multiply_c(f):
+            slots = slice(f * C, (f + 1) * C)
+            nc.vector.quantize_mx(
+                cq[:, slots].bitcast(FP8X4), cqs[:, slots],
+                cg[:, slots, :].rearrange("p m u -> p (m u)").bitcast(BF16),
+            )
+            for n in range(2):
+                bank = banks[2 * (f % 3) + n]
+                nc.tensor.matmul_mx(
+                    bank[:, :C],
+                    lhsT=w2w[:, f, n * P : (n + 1) * P].bitcast(FP8X4),
+                    lhsT_scale=w2s[:, f, n * P : (n + 1) * P],
+                    rhs=cq[:, slots].bitcast(FP8X4),
+                    rhs_scale=cqs[:, slots],
+                    start=True,
+                    stop=True,
+                )
+                nc.scalar.copy(y[n][:, slots], bank[:, :C])
+
+        for f in range(E):
+            gather_c(f, 0)
+            if f > 0:
+                multiply_c(f - 1)
+            gather_c(f, 1)
+        multiply_c(E - 1)
+
+        part = [[sb.tile([P, T], F32, name=f"part{n}_{r}", align_bytes=64) for r in range(2)] for n in range(2)]
+        res = [sb.tile([P, T], F32, name=f"res{n}", align_bytes=64) for n in range(2)]
+
+        def finish(n, lo, hi):
+            nc.vector.tensor_add(res[n][:, lo:hi], part[n][0][:, lo:hi], part[n][1][:, lo:hi])
+            nc.sync.dma_start(out[n * P : (n + 1) * P, lo:hi], res[n][:, lo:hi])
+
+        for i, (n, lo, hi) in enumerate(OUT_RUNS):
+            for r in range(2):
+                nc.vector.tensor_tensor(
+                    part[n][r][:, lo:hi], y[n][:].indirect(entries(pos_2[r], lo, hi)), g2[:, r, lo:hi], MULT
+                )
+                if r == 0 and i > 0:
+                    finish(*OUT_RUNS[i - 1])
+        finish(*OUT_RUNS[-1])

@@ -21,7 +21,9 @@ RELU = mybir.ActivationFunctionType.Relu
 X_PLANE = 8
 EXPERT_RUNS_1 = ((0,), (1,), (2, 3), (4,), (5,))
 TOKEN_RUNS_1 = ((0, 1, 2), (3, 4), (5,))
-OUT_RUNS = ((0, 0, 768), (1, 0, 512), (1, 512, 768))
+SLOT_RUNS_2 = ((0, 256), (256, 768), (768, 1280), (1280, 1408), (1408, 1536))
+OUT_RUNS = ((0, 0, 512), (0, 512, 768), (1, 0, 512), (1, 512, 768))
+TURNED_RUNS = 2
 
 
 def entries(lst, first, last):
@@ -96,7 +98,8 @@ def tile_moe_ser_relu_kernel(
             load_w1_words(2 * g, 2 * g + 2)
         pos_1 = [load_list(pos1, "pos1_t"), load_list(pos2, "pos2_t")]
         g1 = sb.tile([P, 2, T], F32, name="g1")
-        nc.sync.dma_start(g1[:], gate1.rearrange("r p t -> p r t"))
+        for lo in (0, T // 2):
+            nc.sync.dma_start(g1[:, :, lo : lo + T // 2], gate1.rearrange("r p t -> p r t")[:, :, lo : lo + T // 2])
         offs2_t = load_list(offs2, "offs2_t")
         w2w = sb.tile([P, E, N], U32, name="w2w", align_bytes=64)
         nc.sync.dma_start(w2w[:].bitcast(I32), w2_words.rearrange("e s p n d -> p (e s) (n d)").bitcast(I32))
@@ -107,40 +110,34 @@ def tile_moe_ser_relu_kernel(
         g2 = sb.tile([P, 2, T], F32, name="g2")
         nc.sync.dma_start(g2[:], gate2.rearrange("r p t -> p r t"))
 
-        xg = [sb.tile([P, S], U32, name=f"xg{s}", align_bytes=64) for s in range(2)]
-        xgs = sb.tile([P, S], U8, name="xgs", align_bytes=64)
+        xg = [[sb.tile([P, 2 * C], U32, name=f"xg{b}_{s}", align_bytes=64) for s in range(2)] for b in range(2)]
+        xgs = [sb.tile([P, 2 * C], U8, name=f"xgs{b}", align_bytes=64) for b in range(2)]
         h = [sb.tile([P, S], F32, name=f"h{j}", align_bytes=64) for j in range(4)]
         for run, experts in enumerate(EXPERT_RUNS_1):
             lo, hi = experts[0] * C, (experts[-1] + 1) * C
             picked = entries(offs_t, lo, hi)
-            nc.vector.tensor_copy(xg[0][:, lo:hi], xw[0][:].indirect(picked))
-            nc.vector.tensor_copy(xgs[:, lo:hi], xs[:].indirect(picked))
-            nc.vector.tensor_copy(xg[1][:, lo:hi], xw[1][:].indirect(picked))
-            acc = banks[4 * (run % 2) : 4 * (run % 2) + 4]
-
-            def one_pass(e, s, j):
-                a = 2 * (e % 2) + s
-                slots = slice(e * C, (e + 1) * C)
-                cols = slice(j * P, (j + 1) * P)
-                nc.tensor.matmul_mx(
-                    acc[j][:, e * C - lo : (e + 1) * C - lo],
-                    lhsT=w1w[e // 2][:, a, cols].bitcast(FP8X4),
-                    lhsT_scale=w1s[4 * a : P, e // 2, cols],
-                    rhs=xg[s][:, slots].bitcast(FP8X4),
-                    rhs_scale=xgs[X_PLANE + 4 * s : P, slots],
-                    start=(s == 0),
-                    stop=(s == 1),
-                )
-
-            if len(experts) == 1:
-                for j in range(4):
-                    one_pass(experts[0], 0, j)
-            for j in range(4):
-                for e in experts:
-                    if len(experts) > 1:
-                        one_pass(e, 0, j)
-                    one_pass(e, 1, j)
-                nc.scalar.activation(h[j][:, lo:hi], acc[j][:, : hi - lo], RELU)
+            words, scales = xg[run % 2], xgs[run % 2]
+            nc.vector.tensor_copy(words[0][:, : hi - lo], xw[0][:].indirect(picked))
+            nc.vector.tensor_copy(scales[:, : hi - lo], xs[:].indirect(picked))
+            nc.vector.tensor_copy(words[1][:, : hi - lo], xw[1][:].indirect(picked))
+            for e in experts:
+                acc = banks[4 * (e % 2) : 4 * (e % 2) + 4]
+                slots = slice(e * C - lo, (e + 1) * C - lo)
+                for s in range(2):
+                    a = 2 * (e % 2) + s
+                    for j in range(4):
+                        cols = slice(j * P, (j + 1) * P)
+                        nc.tensor.matmul_mx(
+                            acc[j][:, :C],
+                            lhsT=w1w[e // 2][:, a, cols].bitcast(FP8X4),
+                            lhsT_scale=w1s[4 * a : P, e // 2, cols],
+                            rhs=words[s][:, slots].bitcast(FP8X4),
+                            rhs_scale=scales[X_PLANE + 4 * s : P, slots],
+                            start=(s == 0),
+                            stop=(s == 1),
+                        )
+                        if s == 1:
+                            nc.scalar.activation(h[j][:, e * C : (e + 1) * C], acc[j][:, :C], RELU)
 
         prod = [[sb.tile([P, T], F32, name=f"prod{j}_{r}", align_bytes=64) for r in range(2)] for j in range(4)]
         c_rows = [sb.tile([P, 2, P, 2], BF16, name=f"c_rows{t}", align_bytes=64) for t in range(T // P)]
@@ -173,59 +170,102 @@ def tile_moe_ser_relu_kernel(
             for t in tiles:
                 if t != last_tile:
                     nc.scalar.copy(c_rows[t][:], banks[t][:].rearrange("t (p u e) -> t u p e", u=2, e=2))
-                back = banks[6 + t % 2]
+                back = [banks[6 + u] if t == last_tile else banks[6 + t % 2] for u in range(2)]
                 for u in range(2):
                     nc.tensor.transpose(
-                        back[:, u * P : (u + 1) * P],
+                        back[u][:, u * P : (u + 1) * P],
                         c_rows[t][:, u].rearrange("t p e -> t (p e)").bitcast(F32),
                         ident[:],
                     )
-                nc.scalar.copy(
-                    c_pairs[:, :, t * P : (t + 1) * P].bitcast(BF16),
-                    back[:, : 2 * P].bitcast(BF16).rearrange("p (u t) -> p u t", u=2),
-                )
+                if t == last_tile:
+                    for u in range(2):
+                        nc.scalar.copy(
+                            c_pairs[:, u, t * P : (t + 1) * P].bitcast(BF16), back[u][:, u * P : (u + 1) * P].bitcast(BF16)
+                        )
+                else:
+                    nc.scalar.copy(
+                        c_pairs[:, :, t * P : (t + 1) * P].bitcast(BF16),
+                        back[0][:, : 2 * P].bitcast(BF16).rearrange("p (u t) -> p u t", u=2),
+                    )
 
-        cg = sb.tile([P, S, 2], U32, name="cg", align_bytes=64)
+        ring = [sb.tile([P, 4 * C], U32, name=f"ring{b}", align_bytes=64) for b in range(3)]
+        last_run = len(SLOT_RUNS_2) - 1
+
+        def interleaved(run):
+            lo, hi = SLOT_RUNS_2[run]
+            return ring[(2 * run + (run < last_run)) % 3][:, : 2 * (hi - lo)]
+
         cq = sb.tile([P, S], U32, name="cq", align_bytes=64)
         cqs = sb.tile([P, S], U8, name="cqs", align_bytes=64)
         y = [sb.tile([P, S], F32, name=f"y{n}", align_bytes=64) for n in range(2)]
 
-        def gather_c(f, u):
-            lo, hi = f * C, (f + 1) * C
-            nc.vector.tensor_copy(cg[:, lo:hi, u], c_pairs[:, u, :].indirect(entries(offs2_t, lo, hi)))
+        def gather_c(run):
+            lo, hi = SLOT_RUNS_2[run]
+            side_by_side = interleaved(run).rearrange("p (m u) -> p m u", u=2)
+            apart = ring[2 * run % 3][:, : 2 * (hi - lo)].rearrange("p (u m) -> p u m", u=2)
+            for u in range(2):
+                dst = side_by_side[:, :, u] if run == last_run else apart[:, u, :]
+                nc.vector.tensor_copy(dst, c_pairs[:, u, :].indirect(entries(offs2_t, lo, hi)))
+            if run < last_run:
+                nc.scalar.copy(side_by_side, apart.rearrange("p u m -> p m u"))
 
-        def multiply_c(f):
-            slots = slice(f * C, (f + 1) * C)
+        def multiply_c(run):
+            lo, hi = SLOT_RUNS_2[run]
             nc.vector.quantize_mx(
-                cq[:, slots].bitcast(FP8X4), cqs[:, slots],
-                cg[:, slots, :].rearrange("p m u -> p (m u)").bitcast(BF16),
+                cq[:, lo:hi].bitcast(FP8X4), cqs[:, lo:hi],
+                interleaved(run).bitcast(BF16),
             )
             for n in range(2):
-                bank = banks[2 * (f % 3) + n]
-                nc.tensor.matmul_mx(
-                    bank[:, :C],
-                    lhsT=w2w[:, f, n * P : (n + 1) * P].bitcast(FP8X4),
-                    lhsT_scale=w2s[:, f, n * P : (n + 1) * P],
-                    rhs=cq[:, slots].bitcast(FP8X4),
-                    rhs_scale=cqs[:, slots],
-                    start=True,
-                    stop=True,
-                )
-                nc.scalar.copy(y[n][:, slots], bank[:, :C])
+                bank = banks[2 * (run % 3) + n]
+                for first in range(lo, hi, C):
+                    last = min(first + C, hi)
+                    nc.tensor.matmul_mx(
+                        bank[:, first - lo : last - lo],
+                        lhsT=w2w[:, first // C, n * P : (n + 1) * P].bitcast(FP8X4),
+                        lhsT_scale=w2s[:, first // C, n * P : (n + 1) * P],
+                        rhs=cq[:, first:last].bitcast(FP8X4),
+                        rhs_scale=cqs[:, first:last],
+                        start=True,
+                        stop=True,
+                    )
+                nc.scalar.copy(y[n][:, lo:hi], bank[:, : hi - lo])
 
-        for f in range(E):
-            gather_c(f, 0)
-            if f > 0:
-                multiply_c(f - 1)
-            gather_c(f, 1)
-        multiply_c(E - 1)
+        for run in range(len(SLOT_RUNS_2)):
+            gather_c(run)
+            if run > 0:
+                multiply_c(run - 1)
+        multiply_c(len(SLOT_RUNS_2) - 1)
 
         part = [[sb.tile([P, T], F32, name=f"part{n}_{r}", align_bytes=64) for r in range(2)] for n in range(2)]
         res = [sb.tile([P, T], F32, name=f"res{n}", align_bytes=64) for n in range(2)]
+        turned = sb.tile([P, T], F32, name="turned", align_bytes=64)
 
-        def finish(n, lo, hi):
-            nc.vector.tensor_add(res[n][:, lo:hi], part[n][0][:, lo:hi], part[n][1][:, lo:hi])
-            nc.sync.dma_start(out[n * P : (n + 1) * P, lo:hi], res[n][:, lo:hi])
+        def finish(i):
+            n, lo, hi = OUT_RUNS[i]
+            if i >= TURNED_RUNS:
+                nc.vector.tensor_add(res[n][:, lo:hi], part[n][0][:, lo:hi], part[n][1][:, lo:hi])
+                nc.sync.dma_start(out[n * P : (n + 1) * P, lo:hi], res[n][:, lo:hi])
+                return
+            for first in range(lo, hi, 2 * P):
+                there, back = banks[first // P], banks[first // P + 1]
+                cols = slice(first, first + 2 * P)
+                for t in range(2):
+                    for r in range(2):
+                        nc.tensor.matmul(
+                            there[:, t * P : (t + 1) * P],
+                            lhsT=part[n][r][:, first + t * P : first + (t + 1) * P],
+                            rhs=ident[:],
+                            is_transpose=True,
+                            start=(r == 0),
+                            stop=(r == 1),
+                        )
+                nc.scalar.copy(turned[:, cols], there[:, : 2 * P])
+                for t in range(2):
+                    nc.tensor.transpose(
+                        back[:, t * P : (t + 1) * P], turned[:, first + t * P : first + (t + 1) * P], ident[:]
+                    )
+                nc.scalar.copy(res[n][:, cols], back[:, : 2 * P])
+                nc.sync.dma_start(out[n * P : (n + 1) * P, cols], res[n][:, cols])
 
         for i, (n, lo, hi) in enumerate(OUT_RUNS):
             for r in range(2):
@@ -233,5 +273,5 @@ def tile_moe_ser_relu_kernel(
                     part[n][r][:, lo:hi], y[n][:].indirect(entries(pos_2[r], lo, hi)), g2[:, r, lo:hi], MULT
                 )
                 if r == 0 and i > 0:
-                    finish(*OUT_RUNS[i - 1])
-        finish(*OUT_RUNS[-1])
+                    finish(i - 1)
+        finish(len(OUT_RUNS) - 1)

@@ -21,7 +21,7 @@ RELU = mybir.ActivationFunctionType.Relu
 X_PLANE = 8
 EXPERT_RUNS_1 = ((0,), (1,), (2, 3), (4,), (5,))
 TOKEN_RUNS_1 = ((0, 1, 2), (3, 4), (5,))
-SLOT_RUNS_2 = ((0, 256), (256, 768), (768, 1280), (1280, 1408), (1408, 1536))
+SLOT_RUNS_2 = ((0, 512), (512, 1024), (1024, 1280), (1280, 1408), (1408, 1536))
 OUT_RUNS = ((0, 0, 512), (0, 512, 768), (1, 0, 512), (1, 512, 768))
 TURNED_RUNS = 2
 
@@ -56,10 +56,9 @@ def tile_moe_ser_relu_kernel(
         ident = sb.tile([P, P], F32, name="ident", align_bytes=64)
         make_identity(nc, ident[:])
 
-        offs_t = load_list(offs, "offs_t")
         xw = [sb.tile([P, T], U32, name=f"xw{s}", align_bytes=64) for s in range(2)]
         x_passes = x_words.rearrange("s p t d -> s p (t d)")
-        nc.scalar.dma_start(xw[0][:].bitcast(I32), x_passes[0].bitcast(I32))
+        nc.sync.dma_start(xw[0][:].bitcast(I32), x_passes[0].bitcast(I32))
         for q in range(4):
             nc.sync.dma_start(
                 xs_in[32 * q + X_PLANE : 32 * q + X_PLANE + 8, :].bitcast(I32),
@@ -67,6 +66,7 @@ def tile_moe_ser_relu_kernel(
             )
             rows = slice(32 * q, 32 * q + X_PLANE + 8)
             nc.vector.tensor_copy(xs[rows, :].bitcast(I32), xs_in[rows, :].bitcast(I32))
+        offs_t = load_list(offs, "offs_t")
         nc.sync.dma_start(xw[1][:].bitcast(I32), x_passes[1].bitcast(I32))
         w1w = [sb.tile([P, 4, H], U32, name=f"w1w{g}", align_bytes=64) for g in range(E // 2)]
         w1_passes = w1_words.rearrange("e s p i d -> p (e s) (i d)")
@@ -161,15 +161,13 @@ def tile_moe_ser_relu_kernel(
                             start=(r == 0),
                             stop=(r == 1),
                         )
-                    if t == last_tile and j >= 2:
+                    if j >= 2:
                         p0, p1 = (0, 96) if j == 2 else (96, 128)
                         nc.scalar.copy(
                             c_rows[t][:, :, p0:p1, :],
                             bank[:, 4 * p0 : 4 * p1].rearrange("t (p u e) -> t u p e", u=2, e=2),
                         )
             for t in tiles:
-                if t != last_tile:
-                    nc.scalar.copy(c_rows[t][:], banks[t][:].rearrange("t (p u e) -> t u p e", u=2, e=2))
                 back = [banks[6 + u] if t == last_tile else banks[6 + t % 2] for u in range(2)]
                 for u in range(2):
                     nc.tensor.transpose(
@@ -180,12 +178,12 @@ def tile_moe_ser_relu_kernel(
                 if t == last_tile:
                     for u in range(2):
                         nc.scalar.copy(
-                            c_pairs[:, u, t * P : (t + 1) * P].bitcast(BF16), back[u][:, u * P : (u + 1) * P].bitcast(BF16)
+                            c_pairs[:, u, t * P : (t + 1) * P].bitcast(F32), back[u][:, u * P : (u + 1) * P]
                         )
                 else:
                     nc.scalar.copy(
-                        c_pairs[:, :, t * P : (t + 1) * P].bitcast(BF16),
-                        back[0][:, : 2 * P].bitcast(BF16).rearrange("p (u t) -> p u t", u=2),
+                        c_pairs[:, :, t * P : (t + 1) * P].bitcast(F32),
+                        back[0][:, : 2 * P].rearrange("p (u t) -> p u t", u=2),
                     )
 
         ring = [sb.tile([P, 4 * C], U32, name=f"ring{b}", align_bytes=64) for b in range(3)]

@@ -19,7 +19,7 @@ MULT = mybir.AluOpType.mult
 RELU = mybir.ActivationFunctionType.Relu
 
 X_PLANE = 8
-EXPERT_RUNS_1 = ((0,), (1,), (2, 3), (4,), (5,))
+EXPERT_RUNS_1 = ((0,), (1, 2), (3,), (4,), (5,))
 TOKEN_RUNS_1 = ((0, 1, 2), (3, 4), (5,))
 SLOT_RUNS_2 = ((0, 512), (512, 1024), (1024, 1280), (1280, 1408), (1408, 1536))
 OUT_RUNS = ((0, 0, 512), (0, 512, 768), (1, 0, 512), (1, 512, 768))
@@ -58,7 +58,6 @@ def tile_moe_ser_relu_kernel(
 
         xw = [sb.tile([P, T], U32, name=f"xw{s}", align_bytes=64) for s in range(2)]
         x_passes = x_words.rearrange("s p t d -> s p (t d)")
-        nc.sync.dma_start(xw[0][:].bitcast(I32), x_passes[0].bitcast(I32))
         for q in range(4):
             nc.sync.dma_start(
                 xs_in[32 * q + X_PLANE : 32 * q + X_PLANE + 8, :].bitcast(I32),
@@ -67,7 +66,8 @@ def tile_moe_ser_relu_kernel(
             rows = slice(32 * q, 32 * q + X_PLANE + 8)
             nc.vector.tensor_copy(xs[rows, :].bitcast(I32), xs_in[rows, :].bitcast(I32))
         offs_t = load_list(offs, "offs_t")
-        nc.sync.dma_start(xw[1][:].bitcast(I32), x_passes[1].bitcast(I32))
+        for s in range(2):
+            nc.sync.dma_start(xw[s][:].bitcast(I32), x_passes[s].bitcast(I32))
         w1w = [sb.tile([P, 4, H], U32, name=f"w1w{g}", align_bytes=64) for g in range(E // 2)]
         w1_passes = w1_words.rearrange("e s p i d -> p (e s) (i d)")
         w1_rows = w1_scales.rearrange("e s b i -> (e s) b i")
@@ -95,7 +95,8 @@ def tile_moe_ser_relu_kernel(
         load_w1_words(1, 2)
         for g in range(1, E // 2):
             load_w1_scales(g)
-            load_w1_words(2 * g, 2 * g + 2)
+            load_w1_words(2 * g, 2 * g + 1)
+            load_w1_words(2 * g + 1, 2 * g + 2)
         pos_1 = [load_list(pos1, "pos1_t"), load_list(pos2, "pos2_t")]
         g1 = sb.tile([P, 2, T], F32, name="g1")
         for lo in (0, T // 2):

@@ -18,10 +18,11 @@ FP8X4 = mybir.dt.float8_e4m3fn_x4
 MULT = mybir.AluOpType.mult
 RELU = mybir.ActivationFunctionType.Relu
 
-X_PLANE = 8
-EXPERT_RUNS_1 = ((0,), (1, 2), (3,), (4,), (5,))
-TOKEN_RUNS_1 = ((0, 1, 2), (3, 4), (5,))
-SLOT_RUNS_2 = ((0, 512), (512, 1024), (1024, 1280), (1280, 1408), (1408, 1536))
+HALF = S // 2
+WIDE = 1024
+TILES = T // P
+PAIR_RUNS = ((0, 512), (512, 1024), (1024, 1280), (1280, 1536))
+QUANT_RUNS = ((0, 512), (512, 1024), (1024, 1280), (1280, 1408), (1408, 1536))
 OUT_RUNS = ((0, 0, 512), (0, 512, 768), (1, 0, 512), (1, 512, 768))
 TURNED_RUNS = 2
 
@@ -45,62 +46,51 @@ def tile_moe_ser_relu_kernel(
             nc.sync.dma_start(lst[:], src)
             return lst
 
-        xs = sb.tile([P, T], U8, name="xs", align_bytes=64)
-        w1s = sb.tile([P, E // 2, H], U8, name="w1s", align_bytes=64)
+        xs = sb.tile([P, WIDE], U8, name="xs", align_bytes=64)
+        w1s = sb.tile([P, E, H], U8, name="w1s", align_bytes=64)
         w2s = sb.tile([P, E, N], U8, name="w2s", align_bytes=64)
+        xw = [sb.tile([P, WIDE], U32, name="xw0", align_bytes=64), sb.tile([P, T], U32, name="xw1", align_bytes=64)]
+        c_pairs = [sb.tile([P, WIDE], U32, name="c_pairs0", align_bytes=64), sb.tile([P, T], U32, name="c_pairs1", align_bytes=64)]
         nc.gpsimd.memset(xs[:].bitcast(I32), 0)
-        xs_in = sb.tile([P, T], U8, name="xs_in", align_bytes=64)
-        for q in range(4):
-            nc.gpsimd.memset(xs_in[32 * q : 32 * q + X_PLANE, :].bitcast(I32), 0)
+        nc.vector.memset(w1s[:].bitcast(I32), 0)
+        nc.gpsimd.memset(xw[0][:, T:].bitcast(I32), 0)
         nc.vector.memset(w2s[:].bitcast(I32), 0)
+        nc.vector.memset(c_pairs[0][:, T:].bitcast(I32), 0)
         ident = sb.tile([P, P], F32, name="ident", align_bytes=64)
         make_identity(nc, ident[:])
 
-        xw = [sb.tile([P, T], U32, name=f"xw{s}", align_bytes=64) for s in range(2)]
         x_passes = x_words.rearrange("s p t d -> s p (t d)")
+        offs_t = load_list(offs, "offs_t")
+        nc.sync.dma_start(xw[0][:, :T].bitcast(I32), x_passes[0].bitcast(I32))
         for q in range(4):
             nc.sync.dma_start(
-                xs_in[32 * q + X_PLANE : 32 * q + X_PLANE + 8, :].bitcast(I32),
-                x_scales[:, 4 * q : 4 * q + 4, :].bitcast(I32),
+                xs[32 * q : 32 * q + 8, :T].bitcast(I32), x_scales[:, 4 * q : 4 * q + 4, :].bitcast(I32)
             )
-            rows = slice(32 * q, 32 * q + X_PLANE + 8)
-            nc.vector.tensor_copy(xs[rows, :].bitcast(I32), xs_in[rows, :].bitcast(I32))
-        offs_t = load_list(offs, "offs_t")
-        for s in range(2):
-            nc.sync.dma_start(xw[s][:].bitcast(I32), x_passes[s].bitcast(I32))
-        w1w = [sb.tile([P, 4, H], U32, name=f"w1w{g}", align_bytes=64) for g in range(E // 2)]
+        nc.sync.dma_start(xw[1][:].bitcast(I32), x_passes[1].bitcast(I32))
+        w1w = [sb.tile([P, 2, H], U32, name=f"w1w{e}", align_bytes=64) for e in range(E)]
         w1_passes = w1_words.rearrange("e s p i d -> p (e s) (i d)")
-        w1_rows = w1_scales.rearrange("e s b i -> (e s) b i")
+        w1_rows = w1_scales.rearrange("e s b i -> s b e i")
 
-        def load_w1_words(first, last):
-            g, a = first // 2, 2 * (first % 2)
-            nc.sync.dma_start(
-                w1w[g][:, a : a + 2 * (last - first), :].bitcast(I32),
-                w1_passes[:, 2 * first : 2 * last, :].bitcast(I32),
-            )
+        def load_w1_words(e):
+            nc.sync.dma_start(w1w[e][:].bitcast(I32), w1_passes[:, 2 * e : 2 * e + 2, :].bitcast(I32))
 
-        def load_w1_scales(g):
-            if g < E // 2 - 1:
-                spans = [(32 * q, 4 * g, 8, q) for q in range(4)]
-            else:
-                spans = [(0, 4 * g, 4, 0)] + [(32 * q - 16, 4 * g - 4, 8, q) for q in range(1, 4)] + [(P - 16, 4 * g, 4, 3)]
-            for first, pass0, count, q in spans:
+        def load_w1_scales(s):
+            for q in range(4):
+                first = 32 * q + 4 * s
                 nc.sync.dma_start(
-                    w1s[first : first + 4 * count, g, :].bitcast(I32),
-                    w1_rows[pass0 : pass0 + count, 4 * q : 4 * q + 4, :].bitcast(I32),
+                    w1s[first : first + 4, :, :].bitcast(I32), w1_rows[s, 4 * q : 4 * q + 4].bitcast(I32)
                 )
 
-        load_w1_words(0, 1)
+        load_w1_words(0)
         load_w1_scales(0)
-        load_w1_words(1, 2)
-        for g in range(1, E // 2):
-            load_w1_scales(g)
-            load_w1_words(2 * g, 2 * g + 1)
-            load_w1_words(2 * g + 1, 2 * g + 2)
+        load_w1_words(1)
+        load_w1_scales(1)
+        for e in range(2, E):
+            load_w1_words(e)
         pos_1 = [load_list(pos1, "pos1_t"), load_list(pos2, "pos2_t")]
         g1 = sb.tile([P, 2, T], F32, name="g1")
-        for lo in (0, T // 2):
-            nc.sync.dma_start(g1[:, :, lo : lo + T // 2], gate1.rearrange("r p t -> p r t")[:, :, lo : lo + T // 2])
+        for r in range(2):
+            nc.sync.dma_start(g1[:, r, :], gate1[r])
         offs2_t = load_list(offs2, "offs2_t")
         w2w = sb.tile([P, E, N], U32, name="w2w", align_bytes=64)
         nc.sync.dma_start(w2w[:].bitcast(I32), w2_words.rearrange("e s p n d -> p (e s) (n d)").bitcast(I32))
@@ -111,129 +101,185 @@ def tile_moe_ser_relu_kernel(
         g2 = sb.tile([P, 2, T], F32, name="g2")
         nc.sync.dma_start(g2[:], gate2.rearrange("r p t -> p r t"))
 
-        xg = [[sb.tile([P, 2 * C], U32, name=f"xg{b}_{s}", align_bytes=64) for s in range(2)] for b in range(2)]
-        xgs = [sb.tile([P, 2 * C], U8, name=f"xgs{b}", align_bytes=64) for b in range(2)]
+        shift = HALF - C
+        xg0 = sb.tile([P, HALF + shift], U32, name="xg0", align_bytes=64)
+        xgs = sb.tile([P, HALF + shift], U8, name="xgs", align_bytes=64)
+        xg1 = sb.tile([P, HALF], U32, name="xg1", align_bytes=64)
         h = [sb.tile([P, S], F32, name=f"h{j}", align_bytes=64) for j in range(4)]
-        for run, experts in enumerate(EXPERT_RUNS_1):
-            lo, hi = experts[0] * C, (experts[-1] + 1) * C
-            picked = entries(offs_t, lo, hi)
-            words, scales = xg[run % 2], xgs[run % 2]
-            nc.vector.tensor_copy(words[0][:, : hi - lo], xw[0][:].indirect(picked))
-            nc.vector.tensor_copy(scales[:, : hi - lo], xs[:].indirect(picked))
-            nc.vector.tensor_copy(words[1][:, : hi - lo], xw[1][:].indirect(picked))
-            for e in experts:
-                acc = banks[4 * (e % 2) : 4 * (e % 2) + 4]
-                slots = slice(e * C - lo, (e + 1) * C - lo)
+        h_rows = [sb.tile([P, 2, 2, P], F32, name=f"h_rows{e}", align_bytes=64) for e in range(E)]
+
+        def place(e, s):
+            return (e % 3) * C + (shift if (e < 3 and s == 0) else 0)
+
+        def gather_first(half):
+            picked = entries(offs_t, half * HALF, (half + 1) * HALF)
+            first = place(3 * half, 0)
+            nc.vector.tensor_copy(xg0[:, first : first + HALF], xw[0][:].indirect(picked))
+            nc.vector.tensor_copy(xgs[:, first : first + HALF], xs[:].indirect(picked))
+
+        def gather_second(e0, e1):
+            nc.vector.tensor_copy(
+                xg1[:, place(e0, 1) : place(e1 - 1, 1) + C], xw[1][:].indirect(entries(offs_t, e0 * C, e1 * C))
+            )
+
+        def tokens_of(e, s, first, count):
+            words = (xg0, xg1)[s][:, place(e, s) + first : place(e, s) + first + count]
+            return words.bitcast(FP8X4), xgs[4 * s : P, place(e, 0) + first : place(e, 0) + first + count]
+
+        def weights_of(e, s, first, count):
+            return w1w[e][:, s, first : first + count].bitcast(FP8X4), w1s[4 * s : P, e, first : first + count]
+
+        def mx_pass(acc, still, moving, s):
+            nc.tensor.matmul_mx(
+                acc, lhsT=still[0], lhsT_scale=still[1], rhs=moving[0], rhs_scale=moving[1],
+                start=(s == 0), stop=(s == 1),
+            )
+
+        def low_pass(e, j, s, acc):
+            mx_pass(acc, weights_of(e, s, j * P, P), tokens_of(e, s, 0, C), s)
+
+        def high_pass(e, half, s, acc):
+            mx_pass(acc, tokens_of(e, s, half * P, P), weights_of(e, s, 2 * P, 2 * P), s)
+
+        def low_out(j, e0, e1, acc):
+            nc.scalar.activation(h[j][:, e0 * C : e1 * C], acc, RELU)
+
+        def low_rows(j, experts, bank):
+            for n, e in enumerate(experts):
                 for s in range(2):
-                    a = 2 * (e % 2) + s
-                    for j in range(4):
-                        cols = slice(j * P, (j + 1) * P)
-                        nc.tensor.matmul_mx(
-                            acc[j][:, :C],
-                            lhsT=w1w[e // 2][:, a, cols].bitcast(FP8X4),
-                            lhsT_scale=w1s[4 * a : P, e // 2, cols],
-                            rhs=words[s][:, slots].bitcast(FP8X4),
-                            rhs_scale=scales[X_PLANE + 4 * s : P, slots],
-                            start=(s == 0),
-                            stop=(s == 1),
-                        )
-                        if s == 1:
-                            nc.scalar.activation(h[j][:, e * C : (e + 1) * C], acc[j][:, :C], RELU)
+                    low_pass(e, j, s, bank[:, n * C : (n + 1) * C])
+            low_out(j, experts[0], experts[-1] + 1, bank[:, : len(experts) * C])
+
+        def high_rows(e, bank):
+            for half in range(2):
+                for s in range(2):
+                    high_pass(e, half, s, bank[:, half * C : (half + 1) * C])
+            nc.scalar.activation(
+                h_rows[e][:].rearrange("m u a (p v) -> m u (a p) v", v=2),
+                bank[:].rearrange("m (ap u v) -> m u ap v", u=2, v=2),
+                RELU,
+            )
+
+        def turn_high(e0, u, bank):
+            for e in (e0, e0 + 1):
+                for half in range(2):
+                    col = (2 * (e - e0) + half) * P
+                    nc.tensor.transpose(bank[:, col : col + P], h_rows[e][:, u, half, :], ident[:])
+            nc.scalar.copy(h[2 + u][:, e0 * C : (e0 + 2) * C], bank[:])
+
+        gather_first(0)
+        for j in range(2):
+            low_pass(0, j, 0, banks[j][:, :C])
+        for half in range(2):
+            high_pass(0, half, 0, banks[2 + half][:, :C])
+        gather_second(0, 1)
+        for j in range(2):
+            low_pass(0, j, 1, banks[j][:, :C])
+            low_out(j, 0, 1, banks[j][:, :C])
+        for half in range(2):
+            high_pass(0, half, 1, banks[2 + half][:, :C])
+            nc.scalar.activation(
+                h_rows[0][:, :, half, :].rearrange("m u (p v) -> m u p v", v=2),
+                banks[2 + half][:, :C].rearrange("m (p u v) -> m u p v", u=2, v=2),
+                RELU,
+            )
+        gather_second(1, 3)
+        for j in range(2):
+            low_rows(j, (1, 2), banks[4 + j])
+        for e in (1, 2):
+            high_rows(e, banks[5 + e])
+        gather_first(1)
+        first_rows = {3: banks[0], 4: banks[1], 5: banks[6]}
+        for e in (3, 4, 5):
+            low_pass(e, 0, 0, first_rows[e][:, :C])
+        gather_second(3, 5)
+        for e in (3, 4):
+            low_pass(e, 0, 1, first_rows[e][:, :C])
+            low_out(0, e, e + 1, first_rows[e][:, :C])
+        gather_second(5, 6)
+        low_pass(5, 0, 1, first_rows[5][:, :C])
+        low_out(0, 5, 6, first_rows[5][:, :C])
+        low_rows(1, (3, 4), banks[7])
+        low_rows(1, (5,), banks[0])
+        high_rows(3, banks[1])
+        high_rows(4, banks[6])
+        high_rows(5, banks[0])
+        for u in range(2):
+            turn_high(0, u, banks[(7, 1)[u]])
+            for e0 in (2, 4):
+                turn_high(e0, u, banks[e0 + u])
 
         prod = [[sb.tile([P, T], F32, name=f"prod{j}_{r}", align_bytes=64) for r in range(2)] for j in range(4)]
-        c_rows = [sb.tile([P, 2, P, 2], BF16, name=f"c_rows{t}", align_bytes=64) for t in range(T // P)]
-        c_pairs = sb.tile([P, 2, T], U32, name="c_pairs", align_bytes=64)
-        last_tile = T // P - 1
-        for tiles in TOKEN_RUNS_1:
-            lo, hi = tiles[0] * P, (tiles[-1] + 1) * P
-            for j in range(4):
-                for r in range(2):
-                    nc.vector.tensor_tensor(
-                        prod[j][r][:, lo:hi], h[j][:].indirect(entries(pos_1[r], lo, hi)), g1[:, r, lo:hi], MULT
+        c_rows = [sb.tile([P, 2, P, 2], BF16, name=f"c_rows{t}", align_bytes=64) for t in range(TILES)]
+        for j in range(4):
+            for r in range(2):
+                nc.vector.tensor_tensor(prod[j][r][:], h[j][:].indirect(pos_1[r][:]), g1[:, r, :], MULT)
+                for t in range(TILES):
+                    nc.tensor.matmul(
+                        banks[t][:, j * P : (j + 1) * P],
+                        lhsT=prod[j][r][:, t * P : (t + 1) * P],
+                        rhs=ident[:],
+                        is_transpose=True,
+                        start=(r == 0),
+                        stop=(r == 1),
                     )
-                for t in tiles:
-                    bank = banks[0] if (t == last_tile and j == 3) else banks[t]
-                    for r in range(2):
-                        nc.tensor.matmul(
-                            bank[:, j * P : (j + 1) * P],
-                            lhsT=prod[j][r][:, t * P : (t + 1) * P],
-                            rhs=ident[:],
-                            is_transpose=True,
-                            start=(r == 0),
-                            stop=(r == 1),
-                        )
-                    if j >= 2:
-                        p0, p1 = (0, 96) if j == 2 else (96, 128)
-                        nc.scalar.copy(
-                            c_rows[t][:, :, p0:p1, :],
-                            bank[:, 4 * p0 : 4 * p1].rearrange("t (p u e) -> t u p e", u=2, e=2),
-                        )
-            for t in tiles:
-                back = [banks[6 + u] if t == last_tile else banks[6 + t % 2] for u in range(2)]
-                for u in range(2):
-                    nc.tensor.transpose(
-                        back[u][:, u * P : (u + 1) * P],
-                        c_rows[t][:, u].rearrange("t p e -> t (p e)").bitcast(F32),
-                        ident[:],
-                    )
-                if t == last_tile:
-                    for u in range(2):
-                        nc.scalar.copy(
-                            c_pairs[:, u, t * P : (t + 1) * P].bitcast(F32), back[u][:, u * P : (u + 1) * P]
-                        )
-                else:
+            for t in range(TILES):
+                if j == 1:
                     nc.scalar.copy(
-                        c_pairs[:, :, t * P : (t + 1) * P].bitcast(F32),
-                        back[0][:, : 2 * P].rearrange("p (u t) -> p u t", u=2),
+                        c_rows[t][:, :, : P // 2, :],
+                        banks[t][:, : 2 * P].rearrange("t (p u v) -> t u p v", u=2, v=2),
                     )
+                elif j >= 2:
+                    nc.scalar.copy(
+                        c_rows[t][:, j - 2, P // 2 :, :].rearrange("t p v -> t (p v)"),
+                        banks[t][:, j * P : (j + 1) * P],
+                    )
+            if j >= 2:
+                u = j - 2
+                for t0 in range(0, TILES, 2):
+                    back = banks[6 + (t0 // 2 + u) % 2]
+                    for t in (t0, t0 + 1):
+                        nc.tensor.transpose(
+                            back[:, (t - t0) * P : (t - t0 + 1) * P],
+                            c_rows[t][:, u].rearrange("t p v -> t (p v)").bitcast(F32),
+                            ident[:],
+                        )
+                    nc.scalar.copy(c_pairs[u][:, t0 * P : (t0 + 2) * P].bitcast(F32), back[:, : 2 * P])
 
-        ring = [sb.tile([P, 4 * C], U32, name=f"ring{b}", align_bytes=64) for b in range(3)]
-        last_run = len(SLOT_RUNS_2) - 1
-
-        def interleaved(run):
-            lo, hi = SLOT_RUNS_2[run]
-            return ring[(2 * run + (run < last_run)) % 3][:, : 2 * (hi - lo)]
-
+        apart = sb.tile([P, 2, S], U32, name="apart", align_bytes=64)
+        woven = sb.tile([P, 2 * S], U32, name="woven", align_bytes=64)
         cq = sb.tile([P, S], U32, name="cq", align_bytes=64)
         cqs = sb.tile([P, S], U8, name="cqs", align_bytes=64)
         y = [sb.tile([P, S], F32, name=f"y{n}", align_bytes=64) for n in range(2)]
 
-        def gather_c(run):
-            lo, hi = SLOT_RUNS_2[run]
-            side_by_side = interleaved(run).rearrange("p (m u) -> p m u", u=2)
-            apart = ring[2 * run % 3][:, : 2 * (hi - lo)].rearrange("p (u m) -> p u m", u=2)
-            for u in range(2):
-                dst = side_by_side[:, :, u] if run == last_run else apart[:, u, :]
-                nc.vector.tensor_copy(dst, c_pairs[:, u, :].indirect(entries(offs2_t, lo, hi)))
-            if run < last_run:
-                nc.scalar.copy(side_by_side, apart.rearrange("p u m -> p m u"))
-
-        def multiply_c(run):
-            lo, hi = SLOT_RUNS_2[run]
-            nc.vector.quantize_mx(
-                cq[:, lo:hi].bitcast(FP8X4), cqs[:, lo:hi],
-                interleaved(run).bitcast(BF16),
+        for lo in (0, HALF):
+            nc.vector.tensor_copy(apart[:, 0, lo : lo + HALF], c_pairs[0][:].indirect(entries(offs2_t, lo, lo + HALF)))
+        for lo, hi in PAIR_RUNS:
+            nc.vector.tensor_copy(apart[:, 1, lo:hi], c_pairs[1][:].indirect(entries(offs2_t, lo, hi)))
+            nc.scalar.copy(
+                woven[:, 2 * lo : 2 * hi].rearrange("p (m u) -> p m u", u=2),
+                apart[:, :, lo:hi].rearrange("p u m -> p m u"),
             )
-            for n in range(2):
-                bank = banks[2 * (run % 3) + n]
-                for first in range(lo, hi, C):
-                    last = min(first + C, hi)
-                    nc.tensor.matmul_mx(
-                        bank[:, first - lo : last - lo],
-                        lhsT=w2w[:, first // C, n * P : (n + 1) * P].bitcast(FP8X4),
-                        lhsT_scale=w2s[:, first // C, n * P : (n + 1) * P],
-                        rhs=cq[:, first:last].bitcast(FP8X4),
-                        rhs_scale=cqs[:, first:last],
-                        start=True,
-                        stop=True,
-                    )
-                nc.scalar.copy(y[n][:, lo:hi], bank[:, : hi - lo])
 
-        for run in range(len(SLOT_RUNS_2)):
-            gather_c(run)
-            if run > 0:
-                multiply_c(run - 1)
-        multiply_c(len(SLOT_RUNS_2) - 1)
+        def second_layer(n, lo, hi, acc):
+            for first in range(lo, hi, C):
+                last = min(first + C, hi)
+                nc.tensor.matmul_mx(
+                    acc[:, first - lo : last - lo],
+                    lhsT=w2w[:, first // C, n * P : (n + 1) * P].bitcast(FP8X4),
+                    lhsT_scale=w2s[:, first // C, n * P : (n + 1) * P],
+                    rhs=cq[:, first:last].bitcast(FP8X4),
+                    rhs_scale=cqs[:, first:last],
+                    start=True,
+                    stop=True,
+                )
+            nc.scalar.copy(y[n][:, lo:hi], acc[:, : hi - lo])
+
+        for run, (lo, hi) in enumerate(QUANT_RUNS):
+            nc.vector.quantize_mx(cq[:, lo:hi].bitcast(FP8X4), cqs[:, lo:hi], woven[:, 2 * lo : 2 * hi].bitcast(BF16))
+            second_layer(0, lo, hi, banks[run])
+        for run, lo in enumerate(range(0, S, 2 * C)):
+            second_layer(1, lo, lo + 2 * C, banks[4 + run])
 
         part = [[sb.tile([P, T], F32, name=f"part{n}_{r}", align_bytes=64) for r in range(2)] for n in range(2)]
         res = [sb.tile([P, T], F32, name=f"res{n}", align_bytes=64) for n in range(2)]

@@ -47,12 +47,13 @@ def tile_moe_ser_relu_kernel(
             return lst
 
         xs = sb.tile([P, WIDE], U8, name="xs", align_bytes=64)
-        w1s = sb.tile([P, E, H], U8, name="w1s", align_bytes=64)
+        w1s = [sb.tile([P, E // 2, 2, H], U8, name=f"w1s{half}", align_bytes=64) for half in range(2)]
         w2s = sb.tile([P, E, N], U8, name="w2s", align_bytes=64)
         xw = [sb.tile([P, WIDE], U32, name="xw0", align_bytes=64), sb.tile([P, T], U32, name="xw1", align_bytes=64)]
         c_pairs = [sb.tile([P, WIDE], U32, name="c_pairs0", align_bytes=64), sb.tile([P, T], U32, name="c_pairs1", align_bytes=64)]
         nc.gpsimd.memset(xs[:].bitcast(I32), 0)
-        nc.vector.memset(w1s[:].bitcast(I32), 0)
+        nc.gpsimd.memset(w1s[0][:].bitcast(I32), 0)
+        nc.vector.memset(w1s[1][:].bitcast(I32), 0)
         nc.gpsimd.memset(xw[0][:, T:].bitcast(I32), 0)
         nc.vector.memset(w2s[:].bitcast(I32), 0)
         nc.vector.memset(c_pairs[0][:, T:].bitcast(I32), 0)
@@ -69,23 +70,24 @@ def tile_moe_ser_relu_kernel(
         nc.sync.dma_start(xw[1][:].bitcast(I32), x_passes[1].bitcast(I32))
         w1w = [sb.tile([P, 2, H], U32, name=f"w1w{e}", align_bytes=64) for e in range(E)]
         w1_passes = w1_words.rearrange("e s p i d -> p (e s) (i d)")
-        w1_rows = w1_scales.rearrange("e s b i -> s b e i")
+        w1_rows = w1_scales.rearrange("e s b i -> b (e s) i")
 
         def load_w1_words(e):
             nc.sync.dma_start(w1w[e][:].bitcast(I32), w1_passes[:, 2 * e : 2 * e + 2, :].bitcast(I32))
 
-        def load_w1_scales(s):
+        def load_w1_scales(half):
             for q in range(4):
-                first = 32 * q + 4 * s
                 nc.sync.dma_start(
-                    w1s[first : first + 4, :, :].bitcast(I32), w1_rows[s, 4 * q : 4 * q + 4].bitcast(I32)
+                    w1s[half][32 * q : 32 * q + 4].rearrange("b e s i -> b (e s) i").bitcast(I32),
+                    w1_rows[4 * q : 4 * q + 4, E * half : E * (half + 1), :].bitcast(I32),
                 )
 
         load_w1_words(0)
         load_w1_scales(0)
         load_w1_words(1)
+        load_w1_words(2)
         load_w1_scales(1)
-        for e in range(2, E):
+        for e in range(3, E):
             load_w1_words(e)
         pos_1 = [load_list(pos1, "pos1_t"), load_list(pos2, "pos2_t")]
         g1 = sb.tile([P, 2, T], F32, name="g1")
@@ -111,11 +113,11 @@ def tile_moe_ser_relu_kernel(
         def place(e, s):
             return (e % 3) * C + (shift if (e < 3 and s == 0) else 0)
 
-        def gather_first(half):
-            picked = entries(offs_t, half * HALF, (half + 1) * HALF)
-            first = place(3 * half, 0)
-            nc.vector.tensor_copy(xg0[:, first : first + HALF], xw[0][:].indirect(picked))
-            nc.vector.tensor_copy(xgs[:, first : first + HALF], xs[:].indirect(picked))
+        def gather_first(e0, e1):
+            picked = entries(offs_t, e0 * C, e1 * C)
+            cols = slice(place(e0, 0), place(e1 - 1, 0) + C)
+            nc.vector.tensor_copy(xg0[:, cols], xw[0][:].indirect(picked))
+            nc.vector.tensor_copy(xgs[:, cols], xs[:].indirect(picked))
 
         def gather_second(e0, e1):
             nc.vector.tensor_copy(
@@ -127,7 +129,7 @@ def tile_moe_ser_relu_kernel(
             return words.bitcast(FP8X4), xgs[4 * s : P, place(e, 0) + first : place(e, 0) + first + count]
 
         def weights_of(e, s, first, count):
-            return w1w[e][:, s, first : first + count].bitcast(FP8X4), w1s[4 * s : P, e, first : first + count]
+            return w1w[e][:, s, first : first + count].bitcast(FP8X4), w1s[e // 3][:, e % 3, s, first : first + count]
 
         def mx_pass(acc, still, moving, s):
             nc.tensor.matmul_mx(
@@ -167,47 +169,54 @@ def tile_moe_ser_relu_kernel(
                     nc.tensor.transpose(bank[:, col : col + P], h_rows[e][:, u, half, :], ident[:])
             nc.scalar.copy(h[2 + u][:, e0 * C : (e0 + 2) * C], bank[:])
 
-        gather_first(0)
-        for j in range(2):
-            low_pass(0, j, 0, banks[j][:, :C])
-        for half in range(2):
-            high_pass(0, half, 0, banks[2 + half][:, :C])
+        def open_expert(e):
+            for j in range(2):
+                low_pass(e, j, 0, banks[4 * e + j][:, :C])
+            for half in range(2):
+                high_pass(e, half, 0, banks[4 * e + 2 + half][:, :C])
+
+        def close_expert(e):
+            for j in range(2):
+                low_pass(e, j, 1, banks[4 * e + j][:, :C])
+                low_out(j, e, e + 1, banks[4 * e + j][:, :C])
+            for half in range(2):
+                acc = banks[4 * e + 2 + half][:, :C]
+                high_pass(e, half, 1, acc)
+                nc.scalar.activation(
+                    h_rows[e][:, :, half, :].rearrange("m u (p v) -> m u p v", v=2),
+                    acc.rearrange("m (p u v) -> m u p v", u=2, v=2),
+                    RELU,
+                )
+
+        gather_first(0, 1)
+        open_expert(0)
+        gather_first(1, 3)
+        open_expert(1)
         gather_second(0, 1)
-        for j in range(2):
-            low_pass(0, j, 1, banks[j][:, :C])
-            low_out(j, 0, 1, banks[j][:, :C])
-        for half in range(2):
-            high_pass(0, half, 1, banks[2 + half][:, :C])
-            nc.scalar.activation(
-                h_rows[0][:, :, half, :].rearrange("m u (p v) -> m u p v", v=2),
-                banks[2 + half][:, :C].rearrange("m (p u v) -> m u p v", u=2, v=2),
-                RELU,
-            )
+        close_expert(0)
         gather_second(1, 3)
-        for j in range(2):
-            low_rows(j, (1, 2), banks[4 + j])
-        for e in (1, 2):
-            high_rows(e, banks[5 + e])
-        gather_first(1)
-        first_rows = {3: banks[0], 4: banks[1], 5: banks[6]}
+        close_expert(1)
+        high_rows(2, banks[0])
+        low_rows(1, (2,), banks[1])
+        low_rows(0, (2,), banks[2])
+        gather_first(3, 6)
         for e in (3, 4, 5):
-            low_pass(e, 0, 0, first_rows[e][:, :C])
+            low_pass(e, 0, 0, banks[e - 3][:, :C])
         gather_second(3, 5)
         for e in (3, 4):
-            low_pass(e, 0, 1, first_rows[e][:, :C])
-            low_out(0, e, e + 1, first_rows[e][:, :C])
+            low_pass(e, 0, 1, banks[e - 3][:, :C])
+            low_out(0, e, e + 1, banks[e - 3][:, :C])
         gather_second(5, 6)
-        low_pass(5, 0, 1, first_rows[5][:, :C])
-        low_out(0, 5, 6, first_rows[5][:, :C])
-        low_rows(1, (3, 4), banks[7])
+        low_pass(5, 0, 1, banks[2][:, :C])
+        low_out(0, 5, 6, banks[2][:, :C])
         low_rows(1, (5,), banks[0])
-        high_rows(3, banks[1])
-        high_rows(4, banks[6])
-        high_rows(5, banks[0])
+        low_rows(1, (3, 4), banks[2])
+        high_rows(5, banks[1])
+        high_rows(3, banks[0])
+        high_rows(4, banks[2])
         for u in range(2):
-            turn_high(0, u, banks[(7, 1)[u]])
-            for e0 in (2, 4):
-                turn_high(e0, u, banks[e0 + u])
+            for e0 in (0, 2, 4):
+                turn_high(e0, u, banks[(1, 3, 4, 0, 5, 2)[3 * u + e0 // 2]])
 
         prod = [[sb.tile([P, T], F32, name=f"prod{j}_{r}", align_bytes=64) for r in range(2)] for j in range(4)]
         c_rows = [sb.tile([P, 2, P, 2], BF16, name=f"c_rows{t}", align_bytes=64) for t in range(TILES)]
@@ -261,7 +270,7 @@ def tile_moe_ser_relu_kernel(
                 apart[:, :, lo:hi].rearrange("p u m -> p m u"),
             )
 
-        def second_layer(n, lo, hi, acc):
+        def second_layer(n, lo, hi, acc, copy):
             for first in range(lo, hi, C):
                 last = min(first + C, hi)
                 nc.tensor.matmul_mx(
@@ -273,13 +282,13 @@ def tile_moe_ser_relu_kernel(
                     start=True,
                     stop=True,
                 )
-            nc.scalar.copy(y[n][:, lo:hi], acc[:, : hi - lo])
+            copy(y[n][:, lo:hi], acc[:, : hi - lo])
 
         for run, (lo, hi) in enumerate(QUANT_RUNS):
             nc.vector.quantize_mx(cq[:, lo:hi].bitcast(FP8X4), cqs[:, lo:hi], woven[:, 2 * lo : 2 * hi].bitcast(BF16))
-            second_layer(0, lo, hi, banks[run])
+            second_layer(0, lo, hi, banks[run], nc.scalar.copy if run < 3 else nc.vector.tensor_copy)
         for run, lo in enumerate(range(0, S, 2 * C)):
-            second_layer(1, lo, lo + 2 * C, banks[4 + run])
+            second_layer(1, lo, lo + 2 * C, banks[4 - run], nc.scalar.copy)
 
         part = [[sb.tile([P, T], F32, name=f"part{n}_{r}", align_bytes=64) for r in range(2)] for n in range(2)]
         res = [sb.tile([P, T], F32, name=f"res{n}", align_bytes=64) for n in range(2)]

@@ -87,12 +87,16 @@ def tile_moe_ser_relu_kernel(
         load_w1_words(1)
         load_w1_words(2)
         load_w1_scales(1)
-        for e in range(3, E):
-            load_w1_words(e)
+        w1_first = sb.tile([P, E // 2, 2, P], U32, name="w1_first", align_bytes=64)
+        nc.sync.dma_start(
+            w1_first[:].rearrange("p e s i -> p (e s) i").bitcast(I32), w1_passes[:, E:, : 4 * P].bitcast(I32)
+        )
         pos_1 = [load_list(pos1, "pos1_t"), load_list(pos2, "pos2_t")]
         g1 = sb.tile([P, 2, T], F32, name="g1")
-        for r in range(2):
-            nc.sync.dma_start(g1[:, r, :], gate1[r])
+        nc.sync.dma_start(g1[:, 0, :], gate1[0])
+        for e in range(E // 2, E):
+            nc.sync.dma_start(w1w[e][:, :, P:].bitcast(I32), w1_passes[:, 2 * e : 2 * e + 2, 4 * P :].bitcast(I32))
+        nc.sync.dma_start(g1[:, 1, :], gate1[1])
         offs2_t = load_list(offs2, "offs2_t")
         w2w = sb.tile([P, E, N], U32, name="w2w", align_bytes=64)
         nc.sync.dma_start(w2w[:].bitcast(I32), w2_words.rearrange("e s p n d -> p (e s) (n d)").bitcast(I32))
@@ -129,7 +133,8 @@ def tile_moe_ser_relu_kernel(
             return words.bitcast(FP8X4), xgs[4 * s : P, place(e, 0) + first : place(e, 0) + first + count]
 
         def weights_of(e, s, first, count):
-            return w1w[e][:, s, first : first + count].bitcast(FP8X4), w1s[e // 3][:, e % 3, s, first : first + count]
+            words = w1_first[:, e % 3] if (e >= 3 and first == 0) else w1w[e]
+            return words[:, s, first : first + count].bitcast(FP8X4), w1s[e // 3][:, e % 3, s, first : first + count]
 
         def mx_pass(acc, still, moving, s):
             nc.tensor.matmul_mx(
@@ -200,60 +205,87 @@ def tile_moe_ser_relu_kernel(
         low_rows(1, (2,), banks[1])
         low_rows(0, (2,), banks[2])
         gather_first(3, 6)
-        for e in (3, 4, 5):
-            low_pass(e, 0, 0, banks[e - 3][:, :C])
-        gather_second(3, 5)
         for e in (3, 4):
+            low_pass(e, 0, 0, banks[e - 3][:, :C])
+        for half in range(2):
+            mx_pass(banks[2 + half][:, :P], weights_of(5, 0, 0, P), tokens_of(5, 0, half * P, P), 0)
+        for e in (3, 4):
+            gather_second(e, e + 1)
             low_pass(e, 0, 1, banks[e - 3][:, :C])
             low_out(0, e, e + 1, banks[e - 3][:, :C])
-        gather_second(5, 6)
-        low_pass(5, 0, 1, banks[2][:, :C])
-        low_out(0, 5, 6, banks[2][:, :C])
+        for half in range(2):
+            first = 5 * C + half * P
+            nc.vector.tensor_copy(
+                xg1[:, place(5, 1) + half * P : place(5, 1) + (half + 1) * P],
+                xw[1][:].indirect(entries(offs_t, first, first + P)),
+            )
+            mx_pass(banks[2 + half][:, :P], weights_of(5, 1, 0, P), tokens_of(5, 1, half * P, P), 1)
+            nc.scalar.activation(h[0][:, first : first + P], banks[2 + half][:, :P], RELU)
         low_rows(1, (5,), banks[0])
-        low_rows(1, (3, 4), banks[2])
+        low_rows(1, (3, 4), banks[3])
         high_rows(5, banks[1])
         high_rows(3, banks[0])
-        high_rows(4, banks[2])
+        high_rows(4, banks[3])
         for u in range(2):
             for e0 in (0, 2, 4):
-                turn_high(e0, u, banks[(1, 3, 4, 0, 5, 2)[3 * u + e0 // 2]])
+                turn_high(e0, u, banks[(1, 2, 4, 0, 5, 3)[3 * u + e0 // 2]])
 
         prod = [[sb.tile([P, T], F32, name=f"prod{j}_{r}", align_bytes=64) for r in range(2)] for j in range(4)]
-        c_rows = [sb.tile([P, 2, P, 2], BF16, name=f"c_rows{t}", align_bytes=64) for t in range(TILES)]
-        for j in range(4):
+        c_rows = sb.tile([P, TILES, 2, P, 2], BF16, name="c_rows", align_bytes=64)
+
+        def gather_h(j, r, tiles):
+            lo, hi = tiles[0] * P, (tiles[-1] + 1) * P
+            nc.vector.tensor_tensor(
+                prod[j][r][:, lo:hi], h[j][:].indirect(entries(pos_1[r], lo, hi)), g1[:, r, lo:hi], MULT
+            )
+
+        def turn_prod(j, r, t, acc):
+            nc.tensor.matmul(
+                acc, lhsT=prod[j][r][:, t * P : (t + 1) * P], rhs=ident[:],
+                is_transpose=True, start=(r == 0), stop=(r == 1),
+            )
+
+        def turn_back(u, tiles, bank):
+            for n, t in enumerate(tiles):
+                nc.tensor.transpose(
+                    bank[:, n * P : (n + 1) * P],
+                    c_rows[:, t, u].rearrange("t p v -> t (p v)").bitcast(F32),
+                    ident[:],
+                )
+            nc.scalar.copy(
+                c_pairs[u][:, tiles[0] * P : (tiles[-1] + 1) * P].bitcast(F32), bank[:, : len(tiles) * P]
+            )
+
+        every_tile = range(TILES)
+        for j in range(3):
             for r in range(2):
-                nc.vector.tensor_tensor(prod[j][r][:], h[j][:].indirect(pos_1[r][:]), g1[:, r, :], MULT)
-                for t in range(TILES):
-                    nc.tensor.matmul(
-                        banks[t][:, j * P : (j + 1) * P],
-                        lhsT=prod[j][r][:, t * P : (t + 1) * P],
-                        rhs=ident[:],
-                        is_transpose=True,
-                        start=(r == 0),
-                        stop=(r == 1),
-                    )
-            for t in range(TILES):
+                gather_h(j, r, every_tile)
+                for t in every_tile:
+                    turn_prod(j, r, t, banks[t][:, j * P : (j + 1) * P])
+            for t in every_tile:
                 if j == 1:
                     nc.scalar.copy(
-                        c_rows[t][:, :, : P // 2, :],
+                        c_rows[:, t, :, : P // 2, :],
                         banks[t][:, : 2 * P].rearrange("t (p u v) -> t u p v", u=2, v=2),
                     )
-                elif j >= 2:
+                elif j == 2:
                     nc.scalar.copy(
-                        c_rows[t][:, j - 2, P // 2 :, :].rearrange("t p v -> t (p v)"),
-                        banks[t][:, j * P : (j + 1) * P],
+                        c_rows[:, t, 0, P // 2 :, :].rearrange("t p v -> t (p v)"), banks[t][:, 2 * P : 3 * P]
                     )
-            if j >= 2:
-                u = j - 2
-                for t0 in range(0, TILES, 2):
-                    back = banks[6 + (t0 // 2 + u) % 2]
-                    for t in (t0, t0 + 1):
-                        nc.tensor.transpose(
-                            back[:, (t - t0) * P : (t - t0 + 1) * P],
-                            c_rows[t][:, u].rearrange("t p v -> t (p v)").bitcast(F32),
-                            ident[:],
-                        )
-                    nc.scalar.copy(c_pairs[u][:, t0 * P : (t0 + 2) * P].bitcast(F32), back[:, : 2 * P])
+        turn_back(0, range(0, 3), banks[6])
+        turn_back(0, range(3, 6), banks[7])
+        for run, tiles in enumerate((range(0, 4), range(4, 6))):
+            bank = banks[6 + run]
+            for r in range(2):
+                gather_h(3, r, tiles)
+            for n, t in enumerate(tiles):
+                for r in range(2):
+                    turn_prod(3, r, t, bank[:, n * P : (n + 1) * P])
+            nc.scalar.copy(
+                c_rows[:, tiles[0] : tiles[-1] + 1, 1, P // 2 :, :].rearrange("t a p v -> t a (p v)"),
+                bank[:, : len(tiles) * P].rearrange("t (a m) -> t a m", m=P),
+            )
+            turn_back(1, tiles, banks[run])
 
         apart = sb.tile([P, 2, S], U32, name="apart", align_bytes=64)
         woven = sb.tile([P, 2 * S], U32, name="woven", align_bytes=64)

@@ -21,10 +21,10 @@ RELU = mybir.ActivationFunctionType.Relu
 HALF = S // 2
 WIDE = 1024
 TILES = T // P
-PAIR_RUNS = ((0, 512), (512, 1024), (1024, 1280), (1280, 1536))
-QUANT_RUNS = ((0, 512), (512, 1024), (1024, 1280), (1280, 1408), (1408, 1536))
-OUT_RUNS = ((0, 0, 512), (0, 512, 768), (1, 0, 512), (1, 512, 768))
-TURNED_RUNS = 2
+PAIR_RUNS = ((0, 384), (384, 768), (768, 1024), (1024, 1280), (1280, 1536))
+QUANT_RUNS = ((0, 256), (256, 512), (512, 768), (768, 1024), (1024, 1280), (1280, 1408), (1408, 1536))
+OUT_RUNS = ((0, 0, 512), (0, 512, 768), (1, 0, 256), (1, 256, 640), (1, 640, 768))
+TURNED_RUNS = 3
 
 
 def entries(lst, first, last):
@@ -318,13 +318,13 @@ def tile_moe_ser_relu_kernel(
 
         for run, (lo, hi) in enumerate(QUANT_RUNS):
             nc.vector.quantize_mx(cq[:, lo:hi].bitcast(FP8X4), cqs[:, lo:hi], woven[:, 2 * lo : 2 * hi].bitcast(BF16))
-            second_layer(0, lo, hi, banks[run], nc.scalar.copy if run < 3 else nc.vector.tensor_copy)
+            second_layer(0, lo, hi, banks[run], nc.scalar.copy if run < 4 else nc.vector.tensor_copy)
         for run, lo in enumerate(range(0, S, 2 * C)):
-            second_layer(1, lo, lo + 2 * C, banks[4 - run], nc.scalar.copy)
+            second_layer(1, lo, lo + 2 * C, banks[6 - run], nc.scalar.copy)
 
         part = [[sb.tile([P, T], F32, name=f"part{n}_{r}", align_bytes=64) for r in range(2)] for n in range(2)]
         res = [sb.tile([P, T], F32, name=f"res{n}", align_bytes=64) for n in range(2)]
-        turned = sb.tile([P, T], F32, name="turned", align_bytes=64)
+        turned = [sb.tile([P, T], F32, name=f"turned{n}", align_bytes=64) for n in range(2)]
 
         def finish(i):
             n, lo, hi = OUT_RUNS[i]
@@ -333,7 +333,7 @@ def tile_moe_ser_relu_kernel(
                 nc.sync.dma_start(out[n * P : (n + 1) * P, lo:hi], res[n][:, lo:hi])
                 return
             for first in range(lo, hi, 2 * P):
-                there, back = banks[first // P], banks[first // P + 1]
+                there, back = banks[(n * T + first) // P], banks[(n * T + first) // P + 1]
                 cols = slice(first, first + 2 * P)
                 for t in range(2):
                     for r in range(2):
@@ -345,13 +345,13 @@ def tile_moe_ser_relu_kernel(
                             start=(r == 0),
                             stop=(r == 1),
                         )
-                nc.scalar.copy(turned[:, cols], there[:, : 2 * P])
+                nc.scalar.copy(turned[n][:, cols], there[:, : 2 * P])
                 for t in range(2):
                     nc.tensor.transpose(
-                        back[:, t * P : (t + 1) * P], turned[:, first + t * P : first + (t + 1) * P], ident[:]
+                        back[:, t * P : (t + 1) * P], turned[n][:, first + t * P : first + (t + 1) * P], ident[:]
                     )
                 nc.scalar.copy(res[n][:, cols], back[:, : 2 * P])
-                nc.sync.dma_start(out[n * P : (n + 1) * P, cols], res[n][:, cols])
+                nc.scalar.dma_start(out[n * P : (n + 1) * P, cols], res[n][:, cols])
 
         for i, (n, lo, hi) in enumerate(OUT_RUNS):
             for r in range(2):

@@ -49,12 +49,11 @@ def tile_moe_ser_relu_kernel(
         xs = sb.tile([P, WIDE], U8, name="xs", align_bytes=64)
         w1s = [sb.tile([P, E // 2, 2, H], U8, name=f"w1s{half}", align_bytes=64) for half in range(2)]
         w2s = sb.tile([P, E, N], U8, name="w2s", align_bytes=64)
-        xw = [sb.tile([P, WIDE], U32, name="xw0", align_bytes=64), sb.tile([P, T], U32, name="xw1", align_bytes=64)]
+        xw = sb.tile([P, 2 * T], U32, name="xw", align_bytes=64)
         c_pairs = [sb.tile([P, WIDE], U32, name="c_pairs0", align_bytes=64), sb.tile([P, T], U32, name="c_pairs1", align_bytes=64)]
         nc.gpsimd.memset(xs[:].bitcast(I32), 0)
-        nc.gpsimd.memset(w1s[0][:].bitcast(I32), 0)
-        nc.vector.memset(w1s[1][:].bitcast(I32), 0)
-        nc.gpsimd.memset(xw[0][:, T:].bitcast(I32), 0)
+        for planes in w1s:
+            nc.vector.memset(planes[:].bitcast(I32), 0)
         nc.vector.memset(w2s[:].bitcast(I32), 0)
         nc.vector.memset(c_pairs[0][:, T:].bitcast(I32), 0)
         ident = sb.tile([P, P], F32, name="ident", align_bytes=64)
@@ -62,12 +61,12 @@ def tile_moe_ser_relu_kernel(
 
         x_passes = x_words.rearrange("s p t d -> s p (t d)")
         offs_t = load_list(offs, "offs_t")
-        nc.sync.dma_start(xw[0][:, :T].bitcast(I32), x_passes[0].bitcast(I32))
+        nc.sync.dma_start(xw[:, :T].bitcast(I32), x_passes[0].bitcast(I32))
         for q in range(4):
             nc.sync.dma_start(
                 xs[32 * q : 32 * q + 8, :T].bitcast(I32), x_scales[:, 4 * q : 4 * q + 4, :].bitcast(I32)
             )
-        nc.sync.dma_start(xw[1][:].bitcast(I32), x_passes[1].bitcast(I32))
+        nc.sync.dma_start(xw[:, T:].bitcast(I32), x_passes[1].bitcast(I32))
         w1w = [sb.tile([P, 2, H], U32, name=f"w1w{e}", align_bytes=64) for e in range(E)]
         w1_passes = w1_words.rearrange("e s p i d -> p (e s) (i d)")
         w1_rows = w1_scales.rearrange("e s b i -> b (e s) i")
@@ -108,7 +107,7 @@ def tile_moe_ser_relu_kernel(
         nc.sync.dma_start(g2[:], gate2.rearrange("r p t -> p r t"))
 
         shift = HALF - C
-        xg0 = sb.tile([P, HALF + shift], U32, name="xg0", align_bytes=64)
+        xg0 = sb.tile([P, S], U32, name="xg0", align_bytes=64)
         xgs = sb.tile([P, HALF + shift], U8, name="xgs", align_bytes=64)
         xg1 = sb.tile([P, HALF], U32, name="xg1", align_bytes=64)
         h = [sb.tile([P, S], F32, name=f"h{j}", align_bytes=64) for j in range(4)]
@@ -120,16 +119,18 @@ def tile_moe_ser_relu_kernel(
         def gather_first(e0, e1):
             picked = entries(offs_t, e0 * C, e1 * C)
             cols = slice(place(e0, 0), place(e1 - 1, 0) + C)
-            nc.vector.tensor_copy(xg0[:, cols], xw[0][:].indirect(picked))
+            window = xw[:, :T] if e0 < 3 else xw[:, :WIDE]
+            nc.vector.tensor_copy(xg0[:, e0 * C : e1 * C], window.indirect(picked))
             nc.vector.tensor_copy(xgs[:, cols], xs[:].indirect(picked))
 
         def gather_second(e0, e1):
             nc.vector.tensor_copy(
-                xg1[:, place(e0, 1) : place(e1 - 1, 1) + C], xw[1][:].indirect(entries(offs_t, e0 * C, e1 * C))
+                xg1[:, place(e0, 1) : place(e1 - 1, 1) + C], xw[:, T:].indirect(entries(offs_t, e0 * C, e1 * C))
             )
 
         def tokens_of(e, s, first, count):
-            words = (xg0, xg1)[s][:, place(e, s) + first : place(e, s) + first + count]
+            start = (e * C, place(e, 1))[s] + first
+            words = (xg0, xg1)[s][:, start : start + count]
             return words.bitcast(FP8X4), xgs[4 * s : P, place(e, 0) + first : place(e, 0) + first + count]
 
         def weights_of(e, s, first, count):
@@ -217,7 +218,7 @@ def tile_moe_ser_relu_kernel(
             first = 5 * C + half * P
             nc.vector.tensor_copy(
                 xg1[:, place(5, 1) + half * P : place(5, 1) + (half + 1) * P],
-                xw[1][:].indirect(entries(offs_t, first, first + P)),
+                xw[:, T:].indirect(entries(offs_t, first, first + P)),
             )
             mx_pass(banks[2 + half][:, :P], weights_of(5, 1, 0, P), tokens_of(5, 1, half * P, P), 1)
             nc.scalar.activation(h[0][:, first : first + P], banks[2 + half][:, :P], RELU)

@@ -69,16 +69,16 @@ def tile_moe_ser_relu_kernel(
         nc.sync.dma_start(xw[:, T:].bitcast(I32), x_passes[1].bitcast(I32))
         w1w = [sb.tile([P, 2, H], U32, name=f"w1w{e}", align_bytes=64) for e in range(E)]
         w1_passes = w1_words.rearrange("e s p i d -> p (e s) (i d)")
-        w1_rows = w1_scales.rearrange("e s b i -> b (e s) i")
+        w1_rows = w1_scales.rearrange("e s (q r) i -> r q (e s) i", r=4)
 
         def load_w1_words(e):
             nc.sync.dma_start(w1w[e][:].bitcast(I32), w1_passes[:, 2 * e : 2 * e + 2, :].bitcast(I32))
 
         def load_w1_scales(half):
-            for q in range(4):
+            for r in range(4):
                 nc.sync.dma_start(
-                    w1s[half][32 * q : 32 * q + 4].rearrange("b e s i -> b (e s) i").bitcast(I32),
-                    w1_rows[4 * q : 4 * q + 4, E * half : E * (half + 1), :].bitcast(I32),
+                    w1s[half][r:P:32].rearrange("q e s i -> q (e s) i").bitcast(I32),
+                    w1_rows[r, :, E * half : E * (half + 1), :].bitcast(I32),
                 )
 
         load_w1_words(0)

@@ -60,8 +60,8 @@ def tile_moe_ser_relu_kernel(
         make_identity(nc, ident[:])
 
         x_passes = x_words.rearrange("s p t d -> s p (t d)")
-        offs_t = load_list(offs, "offs_t")
         nc.sync.dma_start(xw[:, :T].bitcast(I32), x_passes[0].bitcast(I32))
+        offs_t = load_list(offs, "offs_t")
         for q in range(4):
             nc.sync.dma_start(
                 xs[32 * q : 32 * q + 8, :T].bitcast(I32), x_scales[:, 4 * q : 4 * q + 4, :].bitcast(I32)
@@ -240,11 +240,13 @@ def tile_moe_ser_relu_kernel(
                 prod[j][r][:, lo:hi], h[j][:].indirect(entries(pos_1[r], lo, hi)), g1[:, r, lo:hi], MULT
             )
 
-        def turn_prod(j, r, t, acc):
-            nc.tensor.matmul(
-                acc, lhsT=prod[j][r][:, t * P : (t + 1) * P], rhs=ident[:],
-                is_transpose=True, start=(r == 0), stop=(r == 1),
-            )
+        def turn_sums(pair, tiles, bank):
+            for r in range(2):
+                for n, t in enumerate(tiles):
+                    nc.tensor.matmul(
+                        bank[:, n * P : (n + 1) * P], lhsT=pair[r][:, t * P : (t + 1) * P], rhs=ident[:],
+                        is_transpose=True, start=(r == 0 and n == 0), stop=(r == 1 and n == len(tiles) - 1),
+                    )
 
         def turn_back(u, tiles, bank):
             for n, t in enumerate(tiles):
@@ -258,35 +260,38 @@ def tile_moe_ser_relu_kernel(
             )
 
         every_tile = range(TILES)
-        for j in range(3):
+        for j in range(2):
             for r in range(2):
                 gather_h(j, r, every_tile)
-                for t in every_tile:
-                    turn_prod(j, r, t, banks[t][:, j * P : (j + 1) * P])
+            for run, tiles in enumerate((range(0, 3), range(3, 6))):
+                bank = banks[((2, 0), (4, 5))[j][run]]
+                turn_sums(prod[j], tiles, bank)
+                nc.scalar.copy(
+                    c_rows[:, tiles[0] : tiles[-1] + 1, :, 32 * j : 32 * (j + 1), :].rearrange("t a u p v -> t u a p v"),
+                    bank[:, : len(tiles) * P].rearrange("t (a p u v) -> t u a p v", p=32, u=2, v=2),
+                )
+        even_banks = [banks[b] for b in (6, 7, 1, 3, 2, 0)]
+        for r in range(2):
+            gather_h(2, r, every_tile)
             for t in every_tile:
-                if j == 1:
-                    nc.scalar.copy(
-                        c_rows[:, t, :, : P // 2, :],
-                        banks[t][:, : 2 * P].rearrange("t (p u v) -> t u p v", u=2, v=2),
-                    )
-                elif j == 2:
-                    nc.scalar.copy(
-                        c_rows[:, t, 0, P // 2 :, :].rearrange("t p v -> t (p v)"), banks[t][:, 2 * P : 3 * P]
-                    )
-        turn_back(0, range(0, 3), banks[6])
-        turn_back(0, range(3, 6), banks[7])
+                nc.tensor.matmul(
+                    even_banks[t][:, :P], lhsT=prod[2][r][:, t * P : (t + 1) * P], rhs=ident[:],
+                    is_transpose=True, start=(r == 0), stop=(r == 1),
+                )
+        for t in every_tile:
+            nc.scalar.copy(c_rows[:, t, 0, P // 2 :, :].rearrange("t p v -> t (p v)"), even_banks[t][:, :P])
+        turn_back(0, range(0, 3), banks[4])
+        turn_back(0, range(3, 6), banks[5])
         for run, tiles in enumerate((range(0, 4), range(4, 6))):
-            bank = banks[6 + run]
+            bank = banks[(4, 5)[run]]
             for r in range(2):
                 gather_h(3, r, tiles)
-            for n, t in enumerate(tiles):
-                for r in range(2):
-                    turn_prod(3, r, t, bank[:, n * P : (n + 1) * P])
+            turn_sums(prod[3], tiles, bank)
             nc.scalar.copy(
                 c_rows[:, tiles[0] : tiles[-1] + 1, 1, P // 2 :, :].rearrange("t a p v -> t a (p v)"),
                 bank[:, : len(tiles) * P].rearrange("t (a m) -> t a m", m=P),
             )
-            turn_back(1, tiles, banks[run])
+            turn_back(1, tiles, banks[6 + run])
 
         apart = sb.tile([P, 2, S], U32, name="apart", align_bytes=64)
         woven = sb.tile([P, 2 * S], U32, name="woven", align_bytes=64)
@@ -336,16 +341,7 @@ def tile_moe_ser_relu_kernel(
             for first in range(lo, hi, 2 * P):
                 there, back = banks[(n * T + first) // P], banks[(n * T + first) // P + 1]
                 cols = slice(first, first + 2 * P)
-                for t in range(2):
-                    for r in range(2):
-                        nc.tensor.matmul(
-                            there[:, t * P : (t + 1) * P],
-                            lhsT=part[n][r][:, first + t * P : first + (t + 1) * P],
-                            rhs=ident[:],
-                            is_transpose=True,
-                            start=(r == 0),
-                            stop=(r == 1),
-                        )
+                turn_sums(part[n], range(first // P, first // P + 2), there)
                 nc.scalar.copy(turned[n][:, cols], there[:, : 2 * P])
                 for t in range(2):
                     nc.tensor.transpose(

@@ -21,7 +21,7 @@ RELU = mybir.ActivationFunctionType.Relu
 HALF = S // 2
 WIDE = 1024
 TILES = T // P
-PAIR_RUNS = ((0, 384), (384, 768), (768, 1024), (1024, 1280), (1280, 1536))
+PAIR_RUNS = ((0, 256), (256, 640), (640, 1024), (1024, 1280), (1280, 1536))
 QUANT_RUNS = ((0, 256), (256, 512), (512, 768), (768, 1024), (1024, 1280), (1280, 1408), (1408, 1536))
 OUT_RUNS = ((0, 0, 512), (0, 512, 768), (1, 0, 256), (1, 256, 640), (1, 640, 768))
 TURNED_RUNS = 3
@@ -152,21 +152,31 @@ def tile_moe_ser_relu_kernel(
         def low_out(j, e0, e1, acc):
             nc.scalar.activation(h[j][:, e0 * C : e1 * C], acc, RELU)
 
-        def low_rows(j, experts, bank):
-            for n, e in enumerate(experts):
-                for s in range(2):
-                    low_pass(e, j, s, bank[:, n * C : (n + 1) * C])
-            low_out(j, experts[0], experts[-1] + 1, bank[:, : len(experts) * C])
+        def low_group(j, experts, bank):
+            products = [[(weights_of(e, s, j * P, P), tokens_of(e, s, 0, C)) for e in experts] for s in range(2)]
+            return bank, products, lambda: low_out(j, experts[0], experts[-1] + 1, bank[:, : len(experts) * C])
 
-        def high_rows(e, bank):
-            for half in range(2):
-                for s in range(2):
-                    high_pass(e, half, s, bank[:, half * C : (half + 1) * C])
-            nc.scalar.activation(
+        def high_group(e, bank):
+            products = [
+                [(tokens_of(e, s, half * P, P), weights_of(e, s, 2 * P, 2 * P)) for half in range(2)] for s in range(2)
+            ]
+            return bank, products, lambda: nc.scalar.activation(
                 h_rows[e][:].rearrange("m u a (p v) -> m u (a p) v", v=2),
                 bank[:].rearrange("m (ap u v) -> m u ap v", u=2, v=2),
                 RELU,
             )
+
+        def multiply(*groups):
+            for s in range(2):
+                for bank, products, drain in groups:
+                    for n, (still, moving) in enumerate(products[s]):
+                        nc.tensor.matmul_mx(
+                            bank[:, n * C : (n + 1) * C],
+                            lhsT=still[0], lhsT_scale=still[1], rhs=moving[0], rhs_scale=moving[1],
+                            start=(s == 0 and n == 0), stop=(s == 1 and n == len(products[s]) - 1),
+                        )
+                    if s == 1:
+                        drain()
 
         def turn_high(e0, u, bank):
             for e in (e0, e0 + 1):
@@ -202,9 +212,8 @@ def tile_moe_ser_relu_kernel(
         close_expert(0)
         gather_second(1, 3)
         close_expert(1)
-        high_rows(2, banks[0])
-        low_rows(1, (2,), banks[1])
-        low_rows(0, (2,), banks[2])
+        multiply(high_group(2, banks[0]))
+        multiply(low_group(1, (2,), banks[1]), low_group(0, (2,), banks[2]))
         gather_first(3, 6)
         for e in (3, 4):
             low_pass(e, 0, 0, banks[e - 3][:, :C])
@@ -222,11 +231,10 @@ def tile_moe_ser_relu_kernel(
             )
             mx_pass(banks[2 + half][:, :P], weights_of(5, 1, 0, P), tokens_of(5, 1, half * P, P), 1)
             nc.scalar.activation(h[0][:, first : first + P], banks[2 + half][:, :P], RELU)
-        low_rows(1, (5,), banks[0])
-        low_rows(1, (3, 4), banks[3])
-        high_rows(5, banks[1])
-        high_rows(3, banks[0])
-        high_rows(4, banks[3])
+        multiply(low_group(1, (5,), banks[0]), high_group(5, banks[1]))
+        multiply(low_group(1, (3, 4), banks[3]))
+        multiply(high_group(3, banks[0]))
+        multiply(high_group(4, banks[3]))
         for u in range(2):
             for e0 in (0, 2, 4):
                 turn_high(e0, u, banks[(1, 2, 4, 0, 5, 3)[3 * u + e0 // 2]])
@@ -324,7 +332,7 @@ def tile_moe_ser_relu_kernel(
 
         for run, (lo, hi) in enumerate(QUANT_RUNS):
             nc.vector.quantize_mx(cq[:, lo:hi].bitcast(FP8X4), cqs[:, lo:hi], woven[:, 2 * lo : 2 * hi].bitcast(BF16))
-            second_layer(0, lo, hi, banks[run], nc.scalar.copy if run < 4 else nc.vector.tensor_copy)
+            second_layer(0, lo, hi, banks[run], nc.scalar.copy if run < 5 else nc.vector.tensor_copy)
         for run, lo in enumerate(range(0, S, 2 * C)):
             second_layer(1, lo, lo + 2 * C, banks[6 - run], nc.scalar.copy)
 

@@ -16,15 +16,16 @@ U16 = mybir.dt.uint16
 U8 = mybir.dt.uint8
 FP8X4 = mybir.dt.float8_e4m3fn_x4
 MULT = mybir.AluOpType.mult
+ADD = mybir.AluOpType.add
 RELU = mybir.ActivationFunctionType.Relu
+COPY = mybir.ActivationFunctionType.Copy
 
 HALF = S // 2
 WIDE = 1024
-TILES = T // P
-PAIR_RUNS = ((0, 256), (256, 640), (640, 1024), (1024, 1280), (1280, 1536))
-QUANT_RUNS = ((0, 256), (256, 512), (512, 768), (768, 1024), (1024, 1280), (1280, 1408), (1408, 1536))
-OUT_RUNS = ((0, 0, 512), (0, 512, 768), (1, 0, 256), (1, 256, 640), (1, 640, 768))
-TURNED_RUNS = 3
+TV = 512
+TS = T - TV
+RUNS = ((0, 512), (512, 1024), (1024, 1280), (1280, 1408), (1408, 1536))
+OUT_RUNS = ((0, 0, 512), (1, 0, 384), (1, 384, 512))
 
 
 def entries(lst, first, last):
@@ -46,16 +47,23 @@ def tile_moe_ser_relu_kernel(
             nc.sync.dma_start(lst[:], src)
             return lst
 
+        def load_gates(gate, name, first):
+            rows = sb.tile([P, 2, TV], F32, name=f"{name}_rows")
+            nc.sync.dma_start(rows[:], gate[:, :, :TV].rearrange("r p t -> p r t"))
+            cols = [sb.tile([P, (T - first[r]) // P], F32, name=f"{name}_cols{r}") for r in range(2)]
+            with nc.allow_non_contiguous_dma(reason="one gate value a token on the partitions"):
+                for r in range(2):
+                    nc.sync.dma_start(cols[r][:], gate[r, 0, first[r] :].rearrange("(a t) -> t a", t=P))
+            return rows, cols
+
         xs = sb.tile([P, WIDE], U8, name="xs", align_bytes=64)
         w1s = [sb.tile([P, E // 2, 2, H], U8, name=f"w1s{half}", align_bytes=64) for half in range(2)]
         w2s = sb.tile([P, E, N], U8, name="w2s", align_bytes=64)
         xw = sb.tile([P, 2 * T], U32, name="xw", align_bytes=64)
-        c_pairs = [sb.tile([P, WIDE], U32, name="c_pairs0", align_bytes=64), sb.tile([P, T], U32, name="c_pairs1", align_bytes=64)]
         nc.gpsimd.memset(xs[:].bitcast(I32), 0)
         for planes in w1s:
             nc.vector.memset(planes[:].bitcast(I32), 0)
         nc.vector.memset(w2s[:].bitcast(I32), 0)
-        nc.vector.memset(c_pairs[0][:, T:].bitcast(I32), 0)
         ident = sb.tile([P, P], F32, name="ident", align_bytes=64)
         make_identity(nc, ident[:])
 
@@ -86,16 +94,10 @@ def tile_moe_ser_relu_kernel(
         load_w1_words(1)
         load_w1_words(2)
         load_w1_scales(1)
-        w1_first = sb.tile([P, E // 2, 2, P], U32, name="w1_first", align_bytes=64)
-        nc.sync.dma_start(
-            w1_first[:].rearrange("p e s i -> p (e s) i").bitcast(I32), w1_passes[:, E:, : 4 * P].bitcast(I32)
-        )
-        pos_1 = [load_list(pos1, "pos1_t"), load_list(pos2, "pos2_t")]
-        g1 = sb.tile([P, 2, T], F32, name="g1")
-        nc.sync.dma_start(g1[:, 0, :], gate1[0])
         for e in range(E // 2, E):
-            nc.sync.dma_start(w1w[e][:, :, P:].bitcast(I32), w1_passes[:, 2 * e : 2 * e + 2, 4 * P :].bitcast(I32))
-        nc.sync.dma_start(g1[:, 1, :], gate1[1])
+            load_w1_words(e)
+        pos_1 = [load_list(pos1, "pos1_t"), load_list(pos2, "pos2_t")]
+        g1, g1_cols = load_gates(gate1, "g1", (TV, TV))
         offs2_t = load_list(offs2, "offs2_t")
         w2w = sb.tile([P, E, N], U32, name="w2w", align_bytes=64)
         nc.sync.dma_start(w2w[:].bitcast(I32), w2_words.rearrange("e s p n d -> p (e s) (n d)").bitcast(I32))
@@ -103,150 +105,103 @@ def tile_moe_ser_relu_kernel(
         for r in range(4):
             nc.sync.dma_start(w2s[r:P:32, :, :].bitcast(I32), w2_rows[r].bitcast(I32))
         pos_2 = [load_list(pos3, "pos3_t"), load_list(pos4, "pos4_t")]
-        g2 = sb.tile([P, 2, T], F32, name="g2")
-        nc.sync.dma_start(g2[:], gate2.rearrange("r p t -> p r t"))
+        g2, g2_cols = load_gates(gate2, "g2", (TV - P, TV))
 
-        shift = HALF - C
-        xg0 = sb.tile([P, S], U32, name="xg0", align_bytes=64)
-        xgs = sb.tile([P, HALF + shift], U8, name="xgs", align_bytes=64)
-        xg1 = sb.tile([P, HALF], U32, name="xg1", align_bytes=64)
+        xg = sb.tile([P, 7 * C], U32, name="xg", align_bytes=64)
+        xgs = sb.tile([P, 5 * C], U8, name="xgs", align_bytes=64)
         h = [sb.tile([P, S], F32, name=f"h{j}", align_bytes=64) for j in range(4)]
-        h_rows = [sb.tile([P, 2, 2, P], F32, name=f"h_rows{e}", align_bytes=64) for e in range(E)]
+        word_place = ((0, 1, 4, 5, 3, 6), (2, 3, 6, 2, 4, 5))
+        scale_place = (2, 3, 4, 0, 1, 2)
 
-        def place(e, s):
-            return (e % 3) * C + (shift if (e < 3 and s == 0) else 0)
+        def words_at(s, lo, hi):
+            start = word_place[s][lo // C] * C + lo % C
+            return xg[:, start : start + hi - lo]
 
-        def gather_first(e0, e1):
-            picked = entries(offs_t, e0 * C, e1 * C)
-            cols = slice(place(e0, 0), place(e1 - 1, 0) + C)
-            window = xw[:, :T] if e0 < 3 else xw[:, :WIDE]
-            nc.vector.tensor_copy(xg0[:, e0 * C : e1 * C], window.indirect(picked))
-            nc.vector.tensor_copy(xgs[:, cols], xs[:].indirect(picked))
+        def scales_at(s, lo, hi):
+            start = scale_place[lo // C] * C + lo % C
+            return xgs[4 * s : P, start : start + hi - lo]
 
-        def gather_second(e0, e1):
-            nc.vector.tensor_copy(
-                xg1[:, place(e0, 1) : place(e1 - 1, 1) + C], xw[:, T:].indirect(entries(offs_t, e0 * C, e1 * C))
-            )
+        def gather_words(s, lo, hi):
+            window = xw[:, T:] if s == 1 else (xw[:, :WIDE] if lo == 2 * C else xw[:, :T])
+            nc.vector.tensor_copy(words_at(s, lo, hi), window.indirect(entries(offs_t, lo, hi)))
 
-        def tokens_of(e, s, first, count):
-            start = (e * C, place(e, 1))[s] + first
-            words = (xg0, xg1)[s][:, start : start + count]
-            return words.bitcast(FP8X4), xgs[4 * s : P, place(e, 0) + first : place(e, 0) + first + count]
+        def gather_scales(lo, hi):
+            nc.vector.tensor_copy(scales_at(0, lo, hi), xs[:].indirect(entries(offs_t, lo, hi)))
 
-        def weights_of(e, s, first, count):
-            words = w1_first[:, e % 3] if (e >= 3 and first == 0) else w1w[e]
-            return words[:, s, first : first + count].bitcast(FP8X4), w1s[e // 3][:, e % 3, s, first : first + count]
-
-        def mx_pass(acc, still, moving, s):
-            nc.tensor.matmul_mx(
-                acc, lhsT=still[0], lhsT_scale=still[1], rhs=moving[0], rhs_scale=moving[1],
-                start=(s == 0), stop=(s == 1),
-            )
-
-        def low_pass(e, j, s, acc):
-            mx_pass(acc, weights_of(e, s, j * P, P), tokens_of(e, s, 0, C), s)
-
-        def high_pass(e, half, s, acc):
-            mx_pass(acc, tokens_of(e, s, half * P, P), weights_of(e, s, 2 * P, 2 * P), s)
-
-        def low_out(j, e0, e1, acc):
-            nc.scalar.activation(h[j][:, e0 * C : e1 * C], acc, RELU)
-
-        def low_group(j, experts, bank):
-            products = [[(weights_of(e, s, j * P, P), tokens_of(e, s, 0, C)) for e in experts] for s in range(2)]
-            return bank, products, lambda: low_out(j, experts[0], experts[-1] + 1, bank[:, : len(experts) * C])
-
-        def high_group(e, bank):
-            products = [
-                [(tokens_of(e, s, half * P, P), weights_of(e, s, 2 * P, 2 * P)) for half in range(2)] for s in range(2)
-            ]
-            return bank, products, lambda: nc.scalar.activation(
-                h_rows[e][:].rearrange("m u a (p v) -> m u (a p) v", v=2),
-                bank[:].rearrange("m (ap u v) -> m u ap v", u=2, v=2),
-                RELU,
-            )
-
-        def multiply(*groups):
-            for s in range(2):
-                for bank, products, drain in groups:
-                    for n, (still, moving) in enumerate(products[s]):
-                        nc.tensor.matmul_mx(
-                            bank[:, n * C : (n + 1) * C],
-                            lhsT=still[0], lhsT_scale=still[1], rhs=moving[0], rhs_scale=moving[1],
-                            start=(s == 0 and n == 0), stop=(s == 1 and n == len(products[s]) - 1),
-                        )
-                    if s == 1:
-                        drain()
-
-        def turn_high(e0, u, bank):
-            for e in (e0, e0 + 1):
-                for half in range(2):
-                    col = (2 * (e - e0) + half) * P
-                    nc.tensor.transpose(bank[:, col : col + P], h_rows[e][:, u, half, :], ident[:])
-            nc.scalar.copy(h[2 + u][:, e0 * C : (e0 + 2) * C], bank[:])
-
-        def open_expert(e):
-            for j in range(2):
-                low_pass(e, j, 0, banks[4 * e + j][:, :C])
-            for half in range(2):
-                high_pass(e, half, 0, banks[4 * e + 2 + half][:, :C])
-
-        def close_expert(e):
-            for j in range(2):
-                low_pass(e, j, 1, banks[4 * e + j][:, :C])
-                low_out(j, e, e + 1, banks[4 * e + j][:, :C])
-            for half in range(2):
-                acc = banks[4 * e + 2 + half][:, :C]
-                high_pass(e, half, 1, acc)
-                nc.scalar.activation(
-                    h_rows[e][:, :, half, :].rearrange("m u (p v) -> m u p v", v=2),
-                    acc.rearrange("m (p u v) -> m u p v", u=2, v=2),
-                    RELU,
+        def multiply(pieces, bank, s):
+            col = 0
+            for n, (j, lo, hi) in enumerate(pieces):
+                e = lo // C
+                nc.tensor.matmul_mx(
+                    bank[:, col : col + hi - lo],
+                    lhsT=w1w[e][:, s, j * P : (j + 1) * P].bitcast(FP8X4),
+                    lhsT_scale=w1s[e // 3][:, e % 3, s, j * P : (j + 1) * P],
+                    rhs=words_at(s, lo, hi).bitcast(FP8X4),
+                    rhs_scale=scales_at(s, lo, hi),
+                    start=(s == 0 and n == 0),
+                    stop=(s == 1 and n == len(pieces) - 1),
                 )
+                col = col + hi - lo
 
-        gather_first(0, 1)
-        open_expert(0)
-        gather_first(1, 3)
-        open_expert(1)
-        gather_second(0, 1)
-        close_expert(0)
-        gather_second(1, 3)
-        close_expert(1)
-        multiply(high_group(2, banks[0]))
-        multiply(low_group(1, (2,), banks[1]), low_group(0, (2,), banks[2]))
-        gather_first(3, 6)
-        for e in (3, 4):
-            low_pass(e, 0, 0, banks[e - 3][:, :C])
+        def relu_out(pieces, bank):
+            col = 0
+            for j, lo, hi in pieces:
+                nc.scalar.activation(h[j][:, lo:hi], bank[:, col : col + hi - lo], RELU)
+                col = col + hi - lo
+
+        def first_layer(pieces, bank):
+            for s in range(2):
+                multiply(pieces, bank, s)
+            relu_out(pieces, bank)
+
+        def one_expert(e, first_bank):
+            for jj in range(2):
+                first_layer([(j, e * C, (e + 1) * C) for j in (2 * jj, 2 * jj + 1)], banks[first_bank + jj])
+
+        gather_words(0, 0, 2 * C)
+        gather_scales(0, HALF)
+        gather_words(1, 0, 2 * C)
+        one_expert(0, 0)
+        one_expert(1, 2)
+        gather_words(0, 2 * C, 4 * C)
+        gather_words(1, 2 * C, 3 * C)
+        one_expert(2, 4)
+        gather_scales(HALF, S)
+        gather_words(1, 3 * C, 4 * C)
+        one_expert(3, 6)
+        fifth, sixth, mid = 4 * C, 5 * C, 5 * C + P
+        low_rows = [(0, fifth, sixth), (1, fifth, sixth)]
+        third_rows = [(2, fifth, sixth)]
+        gather_words(0, fifth, sixth)
+        multiply(low_rows, banks[0], 0)
+        multiply(third_rows, banks[1], 0)
+        gather_words(1, fifth, sixth)
+        multiply(low_rows, banks[0], 1)
+        relu_out(low_rows, banks[0])
+        multiply(third_rows, banks[1], 1)
+        relu_out(third_rows, banks[1])
+        last_rows = [(3, fifth, sixth), (3, sixth, mid)]
+        gather_words(0, sixth, S)
+        multiply(last_rows, banks[2], 0)
         for half in range(2):
-            mx_pass(banks[2 + half][:, :P], weights_of(5, 0, 0, P), tokens_of(5, 0, half * P, P), 0)
-        for e in (3, 4):
-            gather_second(e, e + 1)
-            low_pass(e, 0, 1, banks[e - 3][:, :C])
-            low_out(0, e, e + 1, banks[e - 3][:, :C])
-        for half in range(2):
-            first = 5 * C + half * P
-            nc.vector.tensor_copy(
-                xg1[:, place(5, 1) + half * P : place(5, 1) + (half + 1) * P],
-                xw[:, T:].indirect(entries(offs_t, first, first + P)),
-            )
-            mx_pass(banks[2 + half][:, :P], weights_of(5, 1, 0, P), tokens_of(5, 1, half * P, P), 1)
-            nc.scalar.activation(h[0][:, first : first + P], banks[2 + half][:, :P], RELU)
-        multiply(low_group(1, (5,), banks[0]), high_group(5, banks[1]))
-        multiply(low_group(1, (3, 4), banks[3]))
-        multiply(high_group(3, banks[0]))
-        multiply(high_group(4, banks[3]))
-        for u in range(2):
-            for e0 in (0, 2, 4):
-                turn_high(e0, u, banks[(1, 2, 4, 0, 5, 3)[3 * u + e0 // 2]])
+            multiply([(0, sixth + half * P, mid + half * P)], banks[3 + half], 0)
+        gather_words(1, sixth, mid)
+        multiply([(0, sixth, mid)], banks[3], 1)
+        relu_out([(0, sixth, mid)], banks[3])
+        multiply(last_rows, banks[2], 1)
+        gather_words(1, mid, S)
+        multiply([(0, mid, S)], banks[4], 1)
+        relu_out([(0, mid, S)], banks[4])
+        nc.vector.tensor_scalar_max(h[3][:, fifth:mid], banks[2][:, : mid - fifth], 0.0)
+        first_layer([(1, sixth, S)], banks[5])
+        first_layer([(2, sixth, S), (3, mid, S)], banks[6])
 
-        prod = [[sb.tile([P, T], F32, name=f"prod{j}_{r}", align_bytes=64) for r in range(2)] for j in range(4)]
-        c_rows = sb.tile([P, TILES, 2, P, 2], BF16, name="c_rows", align_bytes=64)
-
-        def gather_h(j, r, tiles):
-            lo, hi = tiles[0] * P, (tiles[-1] + 1) * P
-            nc.vector.tensor_tensor(
-                prod[j][r][:, lo:hi], h[j][:].indirect(entries(pos_1[r], lo, hi)), g1[:, r, lo:hi], MULT
-            )
+        prod = [[sb.tile([P, TV], F32, name=f"prod{j}_{r}", align_bytes=64) for r in range(2)] for j in range(4)]
+        plain = [[sb.tile([P, TS], F32, name=f"plain{j}_{r}", align_bytes=64) for r in range(2)] for j in range(4)]
+        c_flat = sb.tile([P, TV // P * H], BF16, name="c_flat", align_bytes=64)
+        s_rows = [[sb.tile([P, P, 2], BF16, name=f"s_rows{a}_{u}", align_bytes=64) for u in range(2)] for a in range(2)]
+        scaled = [sb.tile([P, 2, P, 2], F32, name=f"scaled{a}", align_bytes=64) for a in range(2)]
+        c_pairs = sb.tile([P, 2 * T], U32, name="c_pairs", align_bytes=64)
 
         def turn_sums(pair, tiles, bank):
             for r in range(2):
@@ -256,113 +211,178 @@ def tile_moe_ser_relu_kernel(
                         is_transpose=True, start=(r == 0 and n == 0), stop=(r == 1 and n == len(tiles) - 1),
                     )
 
+        def vector_share(j, tiles, bank):
+            lo, hi = tiles[0] * P, (tiles[-1] + 1) * P
+            for r in range(2):
+                nc.vector.tensor_tensor(
+                    prod[j][r][:, lo:hi], h[j][:].indirect(entries(pos_1[r], lo, hi)), g1[:, r, lo:hi], MULT
+                )
+            turn_sums(prod[j], tiles, bank)
+
+        def round_sums(j, tiles, bank):
+            nc.scalar.copy(
+                c_flat[:, tiles[0] * H : (tiles[-1] + 1) * H].rearrange("t (a u j m) -> t j u a m", u=2, j=4, m=64)[:, j]
+                .rearrange("t u a (p v) -> t u a p v", v=2),
+                bank[:, : len(tiles) * P].rearrange("t (a p u v) -> t u a p v", p=32, u=2, v=2),
+            )
+
+        def scalar_share(j, r):
+            nc.scalar.activation(plain[j][r][:], h[j][:].indirect(entries(pos_1[r], TV, T)), COPY)
+            for a in range(2):
+                nc.tensor.transpose(
+                    banks[2 * r + a][:, j * P : (j + 1) * P], plain[j][r][:, a * P : (a + 1) * P], ident[:]
+                )
+
+        def pairs_of(t, u):
+            if t < TV // P:
+                return c_flat[:, t * H + u * 2 * P : t * H + (u + 1) * 2 * P].bitcast(F32)
+            return s_rows[t - TV // P][u][:].rearrange("t p v -> t (p v)").bitcast(F32)
+
         def turn_back(u, tiles, bank):
             for n, t in enumerate(tiles):
-                nc.tensor.transpose(
-                    bank[:, n * P : (n + 1) * P],
-                    c_rows[:, t, u].rearrange("t p v -> t (p v)").bitcast(F32),
-                    ident[:],
-                )
-            nc.scalar.copy(
-                c_pairs[u][:, tiles[0] * P : (tiles[-1] + 1) * P].bitcast(F32), bank[:, : len(tiles) * P]
-            )
+                nc.tensor.transpose(bank[:, n * P : (n + 1) * P], pairs_of(t, u), ident[:])
 
-        every_tile = range(TILES)
-        for j in range(2):
-            for r in range(2):
-                gather_h(j, r, every_tile)
-            for run, tiles in enumerate((range(0, 3), range(3, 6))):
-                bank = banks[((2, 0), (4, 5))[j][run]]
-                turn_sums(prod[j], tiles, bank)
-                nc.scalar.copy(
-                    c_rows[:, tiles[0] : tiles[-1] + 1, :, 32 * j : 32 * (j + 1), :].rearrange("t a u p v -> t u a p v"),
-                    bank[:, : len(tiles) * P].rearrange("t (a p u v) -> t u a p v", p=32, u=2, v=2),
-                )
-        even_banks = [banks[b] for b in (6, 7, 1, 3, 2, 0)]
-        for r in range(2):
-            gather_h(2, r, every_tile)
-            for t in every_tile:
-                nc.tensor.matmul(
-                    even_banks[t][:, :P], lhsT=prod[2][r][:, t * P : (t + 1) * P], rhs=ident[:],
-                    is_transpose=True, start=(r == 0), stop=(r == 1),
-                )
-        for t in every_tile:
-            nc.scalar.copy(c_rows[:, t, 0, P // 2 :, :].rearrange("t p v -> t (p v)"), even_banks[t][:, :P])
-        turn_back(0, range(0, 3), banks[4])
-        turn_back(0, range(3, 6), banks[5])
-        for run, tiles in enumerate((range(0, 4), range(4, 6))):
-            bank = banks[(4, 5)[run]]
-            for r in range(2):
-                gather_h(3, r, tiles)
-            turn_sums(prod[3], tiles, bank)
-            nc.scalar.copy(
-                c_rows[:, tiles[0] : tiles[-1] + 1, 1, P // 2 :, :].rearrange("t a p v -> t a (p v)"),
-                bank[:, : len(tiles) * P].rearrange("t (a m) -> t a m", m=P),
-            )
-            turn_back(1, tiles, banks[6 + run])
+        def keep_pairs(u, tiles, bank, copy):
+            first = u * T + tiles[0] * P
+            copy(c_pairs[:, first : first + len(tiles) * P].bitcast(F32), bank[:, : len(tiles) * P])
 
-        apart = sb.tile([P, 2, S], U32, name="apart", align_bytes=64)
-        woven = sb.tile([P, 2 * S], U32, name="woven", align_bytes=64)
+        four = range(4)
+        vector_share(0, four, banks[7])
+        vector_share(1, four, banks[4])
+        for j in four:
+            scalar_share(j, 0)
+        for a in range(2):
+            nc.scalar.activation(
+                scaled[a][:], banks[a][:].rearrange("t (p u v) -> t u p v", u=2, v=2), COPY,
+                scale=g1_cols[0][:, a : a + 1],
+            )
+        for j in four:
+            scalar_share(j, 1)
+        vector_share(2, four, banks[5])
+        round_sums(0, four, banks[7])
+        round_sums(1, four, banks[4])
+        round_sums(2, four, banks[5])
+        vector_share(3, range(0, 2), banks[7])
+        round_sums(3, range(0, 2), banks[7])
+        turn_back(0, range(0, 2), banks[0])
+        vector_share(3, range(2, 3), banks[4])
+        round_sums(3, range(2, 3), banks[4])
+        vector_share(3, range(3, 4), banks[7])
+        round_sums(3, range(3, 4), banks[7])
+        keep_pairs(0, range(0, 2), banks[0], nc.scalar.copy)
+        for u in range(2):
+            for a in range(2):
+                nc.vector.scalar_tensor_tensor(
+                    s_rows[a][u][:], banks[2 + a][:].rearrange("t (p u v) -> t u p v", u=2, v=2)[:, u],
+                    g1_cols[1][:, a : a + 1], scaled[a][:, u], MULT, ADD,
+                )
+        turn_back(0, range(4, 6), banks[4])
+        keep_pairs(0, range(4, 6), banks[4], nc.vector.tensor_copy)
+        turn_back(0, range(2, 4), banks[1])
+        keep_pairs(0, range(2, 4), banks[1], nc.scalar.copy)
+        turn_back(1, four, banks[7])
+        keep_pairs(1, four, banks[7], nc.scalar.copy)
+        turn_back(1, range(4, 6), banks[4])
+        keep_pairs(1, range(4, 6), banks[4], nc.scalar.copy)
+
+        ring = [sb.tile([P, 2 * 512], U32, name=f"ring{b}", align_bytes=64) for b in range(4)]
+        spare = [sb.tile([P, 2 * P], U32, name=f"spare{b}", align_bytes=64) for b in range(2)]
+        apart = [ring[0][:], ring[2][:], ring[1][:], ring[3][:, : 2 * P], ring[3][:, 2 * P :]]
+        woven = [ring[1], ring[3], ring[0], spare[0], spare[1]]
         cq = sb.tile([P, S], U32, name="cq", align_bytes=64)
         cqs = sb.tile([P, S], U8, name="cqs", align_bytes=64)
         y = [sb.tile([P, S], F32, name=f"y{n}", align_bytes=64) for n in range(2)]
 
-        for lo in (0, HALF):
-            nc.vector.tensor_copy(apart[:, 0, lo : lo + HALF], c_pairs[0][:].indirect(entries(offs2_t, lo, lo + HALF)))
-        for lo, hi in PAIR_RUNS:
-            nc.vector.tensor_copy(apart[:, 1, lo:hi], c_pairs[1][:].indirect(entries(offs2_t, lo, hi)))
+        def gather_pairs(run):
+            lo, hi = RUNS[run]
+            width = hi - lo
+            for u in range(2):
+                window = c_pairs[:, T:] if u == 1 else (c_pairs[:, :T] if run == 0 else c_pairs[:])
+                nc.vector.tensor_copy(
+                    apart[run][:, u * width : (u + 1) * width], window.indirect(entries(offs2_t, lo, hi))
+                )
             nc.scalar.copy(
-                woven[:, 2 * lo : 2 * hi].rearrange("p (m u) -> p m u", u=2),
-                apart[:, :, lo:hi].rearrange("p u m -> p m u"),
+                woven[run][:, : 2 * width].rearrange("p (m u) -> p m u", u=2),
+                apart[run][:, : 2 * width].rearrange("p (u m) -> p m u", u=2),
             )
 
-        def second_layer(n, lo, hi, acc, copy):
-            for first in range(lo, hi, C):
-                last = min(first + C, hi)
-                nc.tensor.matmul_mx(
-                    acc[:, first - lo : last - lo],
-                    lhsT=w2w[:, first // C, n * P : (n + 1) * P].bitcast(FP8X4),
-                    lhsT_scale=w2s[:, first // C, n * P : (n + 1) * P],
-                    rhs=cq[:, first:last].bitcast(FP8X4),
-                    rhs_scale=cqs[:, first:last],
-                    start=True,
-                    stop=True,
+        def second_layer(run):
+            lo, hi = RUNS[run]
+            nc.vector.quantize_mx(
+                cq[:, lo:hi].bitcast(FP8X4), cqs[:, lo:hi], woven[run][:, : 2 * (hi - lo)].bitcast(BF16)
+            )
+            for n in range(2):
+                acc = banks[(2 * run + n) % 8]
+                for first in range(lo, hi, C):
+                    last = min(first + C, hi)
+                    nc.tensor.matmul_mx(
+                        acc[:, first - lo : last - lo],
+                        lhsT=w2w[:, first // C, n * P : (n + 1) * P].bitcast(FP8X4),
+                        lhsT_scale=w2s[:, first // C, n * P : (n + 1) * P],
+                        rhs=cq[:, first:last].bitcast(FP8X4),
+                        rhs_scale=cqs[:, first:last],
+                        start=True,
+                        stop=True,
+                    )
+                copy = nc.vector.tensor_copy if (n == 0 and run >= 3) else nc.scalar.copy
+                copy(y[n][:, lo:hi], acc[:, : hi - lo])
+
+        gather_pairs(0)
+        gather_pairs(1)
+        second_layer(0)
+        gather_pairs(2)
+        second_layer(1)
+        gather_pairs(3)
+        gather_pairs(4)
+        for run in (2, 3, 4):
+            second_layer(run)
+
+        part = [[sb.tile([P, TV], F32, name=f"part{n}_{r}", align_bytes=64) for r in range(2)] for n in range(2)]
+        res = [sb.tile([P, TV], F32, name=f"res{n}", align_bytes=64) for n in range(2)]
+        bare = [[sb.tile([P, TS + P], F32, name=f"bare{n}_{r}", align_bytes=64) for r in range(2)] for n in range(2)]
+        gated = [[sb.tile([P, N], F32, name=f"gated{a}_{r}", align_bytes=64) for r in range(2)] for a in range(2)]
+        shared = sb.tile([P, P], F32, name="shared", align_bytes=64)
+        s_res = [sb.tile([P, 2, P], F32, name=f"s_res{a}", align_bytes=64) for a in range(2)]
+
+        for r in range(2):
+            for n in (1, 0):
+                extra = P if (n == 1 and r == 0) else 0
+                nc.scalar.activation(
+                    bare[n][r][:, P - extra :], y[n][:].indirect(entries(pos_2[r], TV - extra, T)), COPY
                 )
-            copy(y[n][:, lo:hi], acc[:, : hi - lo])
-
-        for run, (lo, hi) in enumerate(QUANT_RUNS):
-            nc.vector.quantize_mx(cq[:, lo:hi].bitcast(FP8X4), cqs[:, lo:hi], woven[:, 2 * lo : 2 * hi].bitcast(BF16))
-            second_layer(0, lo, hi, banks[run], nc.scalar.copy if run < 5 else nc.vector.tensor_copy)
-        for run, lo in enumerate(range(0, S, 2 * C)):
-            second_layer(1, lo, lo + 2 * C, banks[6 - run], nc.scalar.copy)
-
-        part = [[sb.tile([P, T], F32, name=f"part{n}_{r}", align_bytes=64) for r in range(2)] for n in range(2)]
-        res = [sb.tile([P, T], F32, name=f"res{n}", align_bytes=64) for n in range(2)]
-        turned = [sb.tile([P, T], F32, name=f"turned{n}", align_bytes=64) for n in range(2)]
+                if extra:
+                    nc.tensor.transpose(banks[6][:, :P], bare[n][r][:, :P], ident[:])
+                for a in range(2):
+                    col = (2 * a + n) * P
+                    nc.tensor.transpose(
+                        banks[2 + r][:, col : col + P], bare[n][r][:, (a + 1) * P : (a + 2) * P], ident[:]
+                    )
+        nc.scalar.activation(shared[:], banks[6][:, :P], COPY, scale=g2_cols[0][:, 0:1])
+        nc.tensor.transpose(banks[7][:, :P], shared[:], ident[:])
+        for r in range(2):
+            for a in range(2):
+                nc.scalar.activation(
+                    gated[a][r][:], banks[2 + r][:, a * N : (a + 1) * N], COPY,
+                    scale=g2_cols[r][:, a + 1 - r : a + 2 - r],
+                )
+        out_blocks = out.rearrange("(n p) t -> p n t", p=P)
+        for a in range(2):
+            turn_sums(gated[a], range(2), banks[4 + a])
+            nc.scalar.copy(s_res[a][:].rearrange("p n t -> p (n t)"), banks[4 + a][:, :N])
+            nc.scalar.dma_start(out_blocks[:, :, TV + a * P : TV + (a + 1) * P], s_res[a][:])
 
         def finish(i):
             n, lo, hi = OUT_RUNS[i]
-            if i >= TURNED_RUNS:
-                nc.vector.tensor_add(res[n][:, lo:hi], part[n][0][:, lo:hi], part[n][1][:, lo:hi])
-                nc.sync.dma_start(out[n * P : (n + 1) * P, lo:hi], res[n][:, lo:hi])
-                return
-            for first in range(lo, hi, 2 * P):
-                there, back = banks[(n * T + first) // P], banks[(n * T + first) // P + 1]
-                cols = slice(first, first + 2 * P)
-                turn_sums(part[n], range(first // P, first // P + 2), there)
-                nc.scalar.copy(turned[n][:, cols], there[:, : 2 * P])
-                for t in range(2):
-                    nc.tensor.transpose(
-                        back[:, t * P : (t + 1) * P], turned[n][:, first + t * P : first + (t + 1) * P], ident[:]
-                    )
-                nc.scalar.copy(res[n][:, cols], back[:, : 2 * P])
-                nc.scalar.dma_start(out[n * P : (n + 1) * P, cols], res[n][:, cols])
+            first = banks[7][:, :P] if i == len(OUT_RUNS) - 1 else part[n][0][:, lo:hi]
+            nc.vector.tensor_add(res[n][:, lo:hi], first, part[n][1][:, lo:hi])
+            nc.sync.dma_start(out[n * P : (n + 1) * P, lo:hi], res[n][:, lo:hi])
 
         for i, (n, lo, hi) in enumerate(OUT_RUNS):
-            for r in range(2):
+            slots = (1,) if i == len(OUT_RUNS) - 1 else (0, 1)
+            for r in slots:
                 nc.vector.tensor_tensor(
                     part[n][r][:, lo:hi], y[n][:].indirect(entries(pos_2[r], lo, hi)), g2[:, r, lo:hi], MULT
                 )
-                if r == 0 and i > 0:
+                if r == slots[0] and i > 0:
                     finish(i - 1)
         finish(len(OUT_RUNS) - 1)

@@ -47,14 +47,12 @@ def tile_moe_ser_relu_kernel(
             nc.sync.dma_start(lst[:], src)
             return lst
 
-        def load_gates(gate, name, first):
-            rows = sb.tile([P, 2, TV], F32, name=f"{name}_rows")
-            nc.sync.dma_start(rows[:], gate[:, :, :TV].rearrange("r p t -> p r t"))
+        def load_gate_columns(gate, name, first):
             cols = [sb.tile([P, (T - first[r]) // P], F32, name=f"{name}_cols{r}") for r in range(2)]
             with nc.allow_non_contiguous_dma(reason="one gate value a token on the partitions"):
                 for r in range(2):
                     nc.sync.dma_start(cols[r][:], gate[r, 0, first[r] :].rearrange("(a t) -> t a", t=P))
-            return rows, cols
+            return cols
 
         xs = sb.tile([P, WIDE], U8, name="xs", align_bytes=64)
         w1s = [sb.tile([P, E // 2, 2, H], U8, name=f"w1s{half}", align_bytes=64) for half in range(2)]
@@ -94,10 +92,17 @@ def tile_moe_ser_relu_kernel(
         load_w1_words(1)
         load_w1_words(2)
         load_w1_scales(1)
-        for e in range(E // 2, E):
-            load_w1_words(e)
-        pos_1 = [load_list(pos1, "pos1_t"), load_list(pos2, "pos2_t")]
-        g1, g1_cols = load_gates(gate1, "g1", (TV, TV))
+        load_w1_words(3)
+        load_w1_words(4)
+        w1_first = sb.tile([P, 2, P], U32, name="w1_first", align_bytes=64)
+        nc.sync.dma_start(w1_first[:].bitcast(I32), w1_passes[:, 2 * E - 2 :, : 4 * P].bitcast(I32))
+        pos_1 = [load_list(pos1, "pos1_t")]
+        g1 = [sb.tile([P, TV], F32, name=f"g1_rows{r}") for r in range(2)]
+        nc.sync.dma_start(g1[0][:], gate1[0, :, :TV])
+        nc.sync.dma_start(w1w[E - 1][:, :, P:].bitcast(I32), w1_passes[:, 2 * E - 2 :, 4 * P :].bitcast(I32))
+        pos_1.append(load_list(pos2, "pos2_t"))
+        nc.sync.dma_start(g1[1][:], gate1[1, :, :TV])
+        g1_cols = load_gate_columns(gate1, "g1", (TV, TV))
         offs2_t = load_list(offs2, "offs2_t")
         w2w = sb.tile([P, E, N], U32, name="w2w", align_bytes=64)
         nc.sync.dma_start(w2w[:].bitcast(I32), w2_words.rearrange("e s p n d -> p (e s) (n d)").bitcast(I32))
@@ -105,12 +110,14 @@ def tile_moe_ser_relu_kernel(
         for r in range(4):
             nc.sync.dma_start(w2s[r:P:32, :, :].bitcast(I32), w2_rows[r].bitcast(I32))
         pos_2 = [load_list(pos3, "pos3_t"), load_list(pos4, "pos4_t")]
-        g2, g2_cols = load_gates(gate2, "g2", (TV - P, TV))
+        g2 = sb.tile([P, 2, TV], F32, name="g2_rows")
+        nc.sync.dma_start(g2[:], gate2[:, :, :TV].rearrange("r p t -> p r t"))
+        g2_cols = load_gate_columns(gate2, "g2", (TV - P, TV))
 
         xg = sb.tile([P, 7 * C], U32, name="xg", align_bytes=64)
         xgs = sb.tile([P, 5 * C], U8, name="xgs", align_bytes=64)
         h = [sb.tile([P, S], F32, name=f"h{j}", align_bytes=64) for j in range(4)]
-        word_place = ((0, 1, 4, 5, 3, 6), (2, 3, 6, 2, 4, 5))
+        word_place = ((0, 1, 5, 6, 3, 4), (2, 3, 4, 2, 5, 6))
         scale_place = (2, 3, 4, 0, 1, 2)
 
         def words_at(s, lo, hi):
@@ -132,9 +139,10 @@ def tile_moe_ser_relu_kernel(
             col = 0
             for n, (j, lo, hi) in enumerate(pieces):
                 e = lo // C
+                words = w1_first if (e == E - 1 and j == 0) else w1w[e]
                 nc.tensor.matmul_mx(
                     bank[:, col : col + hi - lo],
-                    lhsT=w1w[e][:, s, j * P : (j + 1) * P].bitcast(FP8X4),
+                    lhsT=words[:, s, j * P : (j + 1) * P].bitcast(FP8X4),
                     lhsT_scale=w1s[e // 3][:, e % 3, s, j * P : (j + 1) * P],
                     rhs=words_at(s, lo, hi).bitcast(FP8X4),
                     rhs_scale=scales_at(s, lo, hi),
@@ -155,16 +163,20 @@ def tile_moe_ser_relu_kernel(
             relu_out(pieces, bank)
 
         def one_expert(e, first_bank):
+            halves = [[(j, e * C, (e + 1) * C) for j in (2 * jj, 2 * jj + 1)] for jj in range(2)]
+            for s in range(2):
+                for jj in range(2):
+                    multiply(halves[jj], banks[first_bank + jj], s)
             for jj in range(2):
-                first_layer([(j, e * C, (e + 1) * C) for j in (2 * jj, 2 * jj + 1)], banks[first_bank + jj])
+                relu_out(halves[jj], banks[first_bank + jj])
 
         gather_words(0, 0, 2 * C)
         gather_scales(0, HALF)
-        gather_words(1, 0, 2 * C)
+        gather_words(1, 0, C)
         one_expert(0, 0)
+        gather_words(1, C, 3 * C)
         one_expert(1, 2)
         gather_words(0, 2 * C, 4 * C)
-        gather_words(1, 2 * C, 3 * C)
         one_expert(2, 4)
         gather_scales(HALF, S)
         gather_words(1, 3 * C, 4 * C)
@@ -180,22 +192,24 @@ def tile_moe_ser_relu_kernel(
         relu_out(low_rows, banks[0])
         multiply(third_rows, banks[1], 1)
         relu_out(third_rows, banks[1])
-        last_rows = [(3, fifth, sixth), (3, sixth, mid)]
+        late = [(3, fifth, sixth), (0, sixth, mid)]
         gather_words(0, sixth, S)
-        multiply(last_rows, banks[2], 0)
-        for half in range(2):
-            multiply([(0, sixth + half * P, mid + half * P)], banks[3 + half], 0)
+        multiply(late, banks[2], 0)
+        multiply([(0, mid, S)], banks[4], 0)
         gather_words(1, sixth, mid)
-        multiply([(0, sixth, mid)], banks[3], 1)
-        relu_out([(0, sixth, mid)], banks[3])
-        multiply(last_rows, banks[2], 1)
+        multiply(late, banks[2], 1)
         gather_words(1, mid, S)
         multiply([(0, mid, S)], banks[4], 1)
         relu_out([(0, mid, S)], banks[4])
-        nc.vector.tensor_scalar_max(h[3][:, fifth:mid], banks[2][:, : mid - fifth], 0.0)
-        first_layer([(1, sixth, S)], banks[5])
-        first_layer([(2, sixth, S), (3, mid, S)], banks[6])
+        nc.vector.tensor_scalar_max(h[0][:, sixth:mid], banks[2][:, C : C + P], 0.0)
+        nc.vector.tensor_scalar_max(h[3][:, fifth:sixth], banks[2][:, :C], 0.0)
+        for s in range(2):
+            for j in range(1, 4):
+                multiply([(j, sixth, S)], banks[4 + j], s)
+        for j in range(1, 4):
+            relu_out([(j, sixth, S)], banks[4 + j])
 
+        later = [banks[b] for b in (0, 1, 5, 6, 4, 3, 2, 7)]
         prod = [[sb.tile([P, TV], F32, name=f"prod{j}_{r}", align_bytes=64) for r in range(2)] for j in range(4)]
         plain = [[sb.tile([P, TS], F32, name=f"plain{j}_{r}", align_bytes=64) for r in range(2)] for j in range(4)]
         c_flat = sb.tile([P, TV // P * H], BF16, name="c_flat", align_bytes=64)
@@ -215,7 +229,7 @@ def tile_moe_ser_relu_kernel(
             lo, hi = tiles[0] * P, (tiles[-1] + 1) * P
             for r in range(2):
                 nc.vector.tensor_tensor(
-                    prod[j][r][:, lo:hi], h[j][:].indirect(entries(pos_1[r], lo, hi)), g1[:, r, lo:hi], MULT
+                    prod[j][r][:, lo:hi], h[j][:].indirect(entries(pos_1[r], lo, hi)), g1[r][:, lo:hi], MULT
                 )
             turn_sums(prod[j], tiles, bank)
 
@@ -230,7 +244,7 @@ def tile_moe_ser_relu_kernel(
             nc.scalar.activation(plain[j][r][:], h[j][:].indirect(entries(pos_1[r], TV, T)), COPY)
             for a in range(2):
                 nc.tensor.transpose(
-                    banks[2 * r + a][:, j * P : (j + 1) * P], plain[j][r][:, a * P : (a + 1) * P], ident[:]
+                    later[2 * (1 - r) + a][:, j * P : (j + 1) * P], plain[j][r][:, a * P : (a + 1) * P], ident[:]
                 )
 
         def pairs_of(t, u):
@@ -247,43 +261,43 @@ def tile_moe_ser_relu_kernel(
             copy(c_pairs[:, first : first + len(tiles) * P].bitcast(F32), bank[:, : len(tiles) * P])
 
         four = range(4)
-        vector_share(0, four, banks[7])
-        vector_share(1, four, banks[4])
-        for j in four:
-            scalar_share(j, 0)
-        for a in range(2):
-            nc.scalar.activation(
-                scaled[a][:], banks[a][:].rearrange("t (p u v) -> t u p v", u=2, v=2), COPY,
-                scale=g1_cols[0][:, a : a + 1],
-            )
+        vector_share(0, four, later[7])
+        vector_share(1, four, later[4])
         for j in four:
             scalar_share(j, 1)
-        vector_share(2, four, banks[5])
-        round_sums(0, four, banks[7])
-        round_sums(1, four, banks[4])
-        round_sums(2, four, banks[5])
-        vector_share(3, range(0, 2), banks[7])
-        round_sums(3, range(0, 2), banks[7])
-        turn_back(0, range(0, 2), banks[0])
-        vector_share(3, range(2, 3), banks[4])
-        round_sums(3, range(2, 3), banks[4])
-        vector_share(3, range(3, 4), banks[7])
-        round_sums(3, range(3, 4), banks[7])
-        keep_pairs(0, range(0, 2), banks[0], nc.scalar.copy)
+        for a in range(2):
+            nc.scalar.activation(
+                scaled[a][:], later[a][:].rearrange("t (p u v) -> t u p v", u=2, v=2), COPY,
+                scale=g1_cols[1][:, a : a + 1],
+            )
+        for j in four:
+            scalar_share(j, 0)
+        vector_share(2, four, later[5])
+        round_sums(0, four, later[7])
+        round_sums(1, four, later[4])
+        round_sums(2, four, later[5])
+        vector_share(3, range(0, 2), later[7])
+        round_sums(3, range(0, 2), later[7])
+        turn_back(0, range(0, 2), later[0])
+        vector_share(3, range(2, 3), later[4])
+        round_sums(3, range(2, 3), later[4])
+        vector_share(3, range(3, 4), later[7])
+        round_sums(3, range(3, 4), later[7])
+        keep_pairs(0, range(0, 2), later[0], nc.scalar.copy)
         for u in range(2):
             for a in range(2):
                 nc.vector.scalar_tensor_tensor(
-                    s_rows[a][u][:], banks[2 + a][:].rearrange("t (p u v) -> t u p v", u=2, v=2)[:, u],
-                    g1_cols[1][:, a : a + 1], scaled[a][:, u], MULT, ADD,
+                    s_rows[a][u][:], later[2 + a][:].rearrange("t (p u v) -> t u p v", u=2, v=2)[:, u],
+                    g1_cols[0][:, a : a + 1], scaled[a][:, u], MULT, ADD,
                 )
-        turn_back(0, range(4, 6), banks[4])
-        keep_pairs(0, range(4, 6), banks[4], nc.vector.tensor_copy)
-        turn_back(0, range(2, 4), banks[1])
-        keep_pairs(0, range(2, 4), banks[1], nc.scalar.copy)
-        turn_back(1, four, banks[7])
-        keep_pairs(1, four, banks[7], nc.scalar.copy)
-        turn_back(1, range(4, 6), banks[4])
-        keep_pairs(1, range(4, 6), banks[4], nc.scalar.copy)
+        turn_back(0, range(4, 6), later[4])
+        keep_pairs(0, range(4, 6), later[4], nc.vector.tensor_copy)
+        turn_back(0, range(2, 4), later[1])
+        keep_pairs(0, range(2, 4), later[1], nc.scalar.copy)
+        turn_back(1, four, later[7])
+        keep_pairs(1, four, later[7], nc.scalar.copy)
+        turn_back(1, range(4, 6), later[4])
+        keep_pairs(1, range(4, 6), later[4], nc.scalar.copy)
 
         ring = [sb.tile([P, 2 * 512], U32, name=f"ring{b}", align_bytes=64) for b in range(4)]
         spare = [sb.tile([P, 2 * P], U32, name=f"spare{b}", align_bytes=64) for b in range(2)]

@@ -55,7 +55,7 @@ def tile_moe_ser_relu_kernel(
             return cols
 
         xs = sb.tile([P, WIDE], U8, name="xs", align_bytes=64)
-        w1s = [sb.tile([P, E // 2, 2, H], U8, name=f"w1s{half}", align_bytes=64) for half in range(2)]
+        w1s = [sb.tile([P, E, H], U8, name=f"w1s{s}", align_bytes=64) for s in range(2)]
         w2s = sb.tile([P, E, N], U8, name="w2s", align_bytes=64)
         xw = sb.tile([P, 2 * T], U32, name="xw", align_bytes=64)
         nc.gpsimd.memset(xs[:].bitcast(I32), 0)
@@ -75,25 +75,20 @@ def tile_moe_ser_relu_kernel(
         nc.sync.dma_start(xw[:, T:].bitcast(I32), x_passes[1].bitcast(I32))
         w1w = [sb.tile([P, 2, H], U32, name=f"w1w{e}", align_bytes=64) for e in range(E)]
         w1_passes = w1_words.rearrange("e s p i d -> p (e s) (i d)")
-        w1_rows = w1_scales.rearrange("e s (q r) i -> r q (e s) i", r=4)
+        w1_rows = w1_scales.rearrange("e s (q r) i -> s r q e i", r=4)
 
         def load_w1_words(e):
             nc.sync.dma_start(w1w[e][:].bitcast(I32), w1_passes[:, 2 * e : 2 * e + 2, :].bitcast(I32))
 
-        def load_w1_scales(half):
+        def load_w1_scales(s):
             for r in range(4):
-                nc.sync.dma_start(
-                    w1s[half][r:P:32].rearrange("q e s i -> q (e s) i").bitcast(I32),
-                    w1_rows[r, :, E * half : E * (half + 1), :].bitcast(I32),
-                )
+                nc.sync.dma_start(w1s[s][4 * s + r : P : 32].bitcast(I32), w1_rows[s, r].bitcast(I32))
 
         load_w1_words(0)
-        load_w1_scales(0)
-        load_w1_words(1)
-        load_w1_words(2)
-        load_w1_scales(1)
-        load_w1_words(3)
-        load_w1_words(4)
+        for s in range(2):
+            load_w1_scales(s)
+        for e in range(1, E - 1):
+            load_w1_words(e)
         w1_first = sb.tile([P, 2, P], U32, name="w1_first", align_bytes=64)
         nc.sync.dma_start(w1_first[:].bitcast(I32), w1_passes[:, 2 * E - 2 :, : 4 * P].bitcast(I32))
         pos_1 = [load_list(pos1, "pos1_t")]
@@ -143,7 +138,7 @@ def tile_moe_ser_relu_kernel(
                 nc.tensor.matmul_mx(
                     bank[:, col : col + hi - lo],
                     lhsT=words[:, s, j * P : (j + 1) * P].bitcast(FP8X4),
-                    lhsT_scale=w1s[e // 3][:, e % 3, s, j * P : (j + 1) * P],
+                    lhsT_scale=w1s[s][4 * s : P, e, j * P : (j + 1) * P],
                     rhs=words_at(s, lo, hi).bitcast(FP8X4),
                     rhs_scale=scales_at(s, lo, hi),
                     start=(s == 0 and n == 0),

@@ -109,10 +109,10 @@ def tile_moe_ser_relu_kernel(
         nc.sync.dma_start(g2[:], gate2[:, :, :TV].rearrange("r p t -> p r t"))
         g2_cols = load_gate_columns(gate2, "g2", (TV - P, TV))
 
-        xg = sb.tile([P, 7 * C], U32, name="xg", align_bytes=64)
+        xg = sb.tile([P, 8 * C], U32, name="xg", align_bytes=64)
         xgs = sb.tile([P, 5 * C], U8, name="xgs", align_bytes=64)
         h = [sb.tile([P, S], F32, name=f"h{j}", align_bytes=64) for j in range(4)]
-        word_place = ((0, 1, 5, 6, 3, 4), (2, 3, 4, 2, 5, 6))
+        word_place = ((0, 1, 5, 6, 3, 4), (2, 3, 4, 7, 5, 6))
         scale_place = (2, 3, 4, 0, 1, 2)
 
         def words_at(s, lo, hi):
@@ -173,8 +173,8 @@ def tile_moe_ser_relu_kernel(
         one_expert(1, 2)
         gather_words(0, 2 * C, 4 * C)
         one_expert(2, 4)
-        gather_scales(HALF, S)
         gather_words(1, 3 * C, 4 * C)
+        gather_scales(HALF, S)
         one_expert(3, 6)
         fifth, sixth, mid = 4 * C, 5 * C, 5 * C + P
         low_rows = [(0, fifth, sixth), (1, fifth, sixth)]

@@ -107,7 +107,7 @@ def tile_moe_ser_relu_kernel(
         pos_2 = [load_list(pos3, "pos3_t"), load_list(pos4, "pos4_t")]
         g2 = sb.tile([P, 2, TV], F32, name="g2_rows")
         nc.sync.dma_start(g2[:], gate2[:, :, :TV].rearrange("r p t -> p r t"))
-        g2_cols = load_gate_columns(gate2, "g2", (TV - P, TV))
+        g2_cols = load_gate_columns(gate2, "g2", (TV, TV))
 
         xg = sb.tile([P, 8 * C], U32, name="xg", align_bytes=64)
         xgs = sb.tile([P, 5 * C], U8, name="xgs", align_bytes=64)
@@ -348,31 +348,23 @@ def tile_moe_ser_relu_kernel(
 
         part = [[sb.tile([P, TV], F32, name=f"part{n}_{r}", align_bytes=64) for r in range(2)] for n in range(2)]
         res = [sb.tile([P, TV], F32, name=f"res{n}", align_bytes=64) for n in range(2)]
-        bare = [[sb.tile([P, TS + P], F32, name=f"bare{n}_{r}", align_bytes=64) for r in range(2)] for n in range(2)]
+        bare = [[sb.tile([P, TS], F32, name=f"bare{n}_{r}", align_bytes=64) for r in range(2)] for n in range(2)]
         gated = [[sb.tile([P, N], F32, name=f"gated{a}_{r}", align_bytes=64) for r in range(2)] for a in range(2)]
-        shared = sb.tile([P, P], F32, name="shared", align_bytes=64)
         s_res = [sb.tile([P, 2, P], F32, name=f"s_res{a}", align_bytes=64) for a in range(2)]
 
         for r in range(2):
             for n in (1, 0):
-                extra = P if (n == 1 and r == 0) else 0
-                nc.scalar.activation(
-                    bare[n][r][:, P - extra :], y[n][:].indirect(entries(pos_2[r], TV - extra, T)), COPY
-                )
-                if extra:
-                    nc.tensor.transpose(banks[6][:, :P], bare[n][r][:, :P], ident[:])
+                nc.scalar.activation(bare[n][r][:], y[n][:].indirect(entries(pos_2[r], TV, T)), COPY)
                 for a in range(2):
                     col = (2 * a + n) * P
                     nc.tensor.transpose(
-                        banks[2 + r][:, col : col + P], bare[n][r][:, (a + 1) * P : (a + 2) * P], ident[:]
+                        banks[2 + r][:, col : col + P], bare[n][r][:, a * P : (a + 1) * P], ident[:]
                     )
-        nc.scalar.activation(shared[:], banks[6][:, :P], COPY, scale=g2_cols[0][:, 0:1])
-        nc.tensor.transpose(banks[7][:, :P], shared[:], ident[:])
         for r in range(2):
             for a in range(2):
                 nc.scalar.activation(
                     gated[a][r][:], banks[2 + r][:, a * N : (a + 1) * N], COPY,
-                    scale=g2_cols[r][:, a + 1 - r : a + 2 - r],
+                    scale=g2_cols[r][:, a : a + 1],
                 )
         out_blocks = out.rearrange("(n p) t -> p n t", p=P)
         for a in range(2):
@@ -382,16 +374,19 @@ def tile_moe_ser_relu_kernel(
 
         def finish(i):
             n, lo, hi = OUT_RUNS[i]
-            first = banks[7][:, :P] if i == len(OUT_RUNS) - 1 else part[n][0][:, lo:hi]
-            nc.vector.tensor_add(res[n][:, lo:hi], first, part[n][1][:, lo:hi])
+            nc.vector.tensor_add(res[n][:, lo:hi], part[n][0][:, lo:hi], part[n][1][:, lo:hi])
             nc.sync.dma_start(out[n * P : (n + 1) * P, lo:hi], res[n][:, lo:hi])
 
-        for i, (n, lo, hi) in enumerate(OUT_RUNS):
-            slots = (1,) if i == len(OUT_RUNS) - 1 else (0, 1)
-            for r in slots:
-                nc.vector.tensor_tensor(
-                    part[n][r][:, lo:hi], y[n][:].indirect(entries(pos_2[r], lo, hi)), g2[:, r, lo:hi], MULT
-                )
-                if r == slots[0] and i > 0:
-                    finish(i - 1)
-        finish(len(OUT_RUNS) - 1)
+        def gated_gather(n, r, lo, hi):
+            nc.vector.tensor_tensor(
+                part[n][r][:, lo:hi], y[n][:].indirect(entries(pos_2[r], lo, hi)), g2[:, r, lo:hi], MULT
+            )
+
+        for r in range(2):
+            gated_gather(0, r, 0, TV)
+        gated_gather(1, 0, 0, TV)
+        finish(0)
+        for n, lo, hi in OUT_RUNS[1:]:
+            gated_gather(n, 1, lo, hi)
+        finish(1)
+        finish(2)

@@ -25,7 +25,7 @@ WIDE = 1024
 TV = 512
 TS = T - TV
 RUNS = ((0, 512), (512, 1024), (1024, 1280), (1280, 1408), (1408, 1536))
-OUT_RUNS = ((0, 0, 512), (1, 0, 384), (1, 384, 512))
+OUT_RUNS = ((0, 0, 512), (1, 0, 256), (1, 256, 384), (1, 384, 512))
 
 
 def entries(lst, first, last):
@@ -333,7 +333,7 @@ def tile_moe_ser_relu_kernel(
                         start=True,
                         stop=True,
                     )
-                copy = nc.vector.tensor_copy if (n == 0 and run >= 3) else nc.scalar.copy
+                copy = nc.vector.tensor_copy if (run == 3 or (run, n) == (4, 0)) else nc.scalar.copy
                 copy(y[n][:, lo:hi], acc[:, : hi - lo])
 
         gather_pairs(0)
@@ -352,20 +352,18 @@ def tile_moe_ser_relu_kernel(
         gated = [[sb.tile([P, N], F32, name=f"gated{a}_{r}", align_bytes=64) for r in range(2)] for a in range(2)]
         s_res = [sb.tile([P, 2, P], F32, name=f"s_res{a}", align_bytes=64) for a in range(2)]
 
-        for r in range(2):
+        turned = [[banks[2][:, a * N : (a + 1) * N], banks[3 + 3 * a][:, :N]] for a in range(2)]
+        for r, tiles in ((0, range(2)), (1, range(1)), (1, range(1, 2))):
+            lo, hi = tiles[0] * P, (tiles[-1] + 1) * P
             for n in (1, 0):
-                nc.scalar.activation(bare[n][r][:], y[n][:].indirect(entries(pos_2[r], TV, T)), COPY)
-                for a in range(2):
-                    col = (2 * a + n) * P
+                nc.scalar.activation(bare[n][r][:, lo:hi], y[n][:].indirect(entries(pos_2[r], TV + lo, TV + hi)), COPY)
+                for a in tiles:
                     nc.tensor.transpose(
-                        banks[2 + r][:, col : col + P], bare[n][r][:, a * P : (a + 1) * P], ident[:]
+                        turned[a][r][:, n * P : (n + 1) * P], bare[n][r][:, a * P : (a + 1) * P], ident[:]
                     )
-        for r in range(2):
-            for a in range(2):
-                nc.scalar.activation(
-                    gated[a][r][:], banks[2 + r][:, a * N : (a + 1) * N], COPY,
-                    scale=g2_cols[r][:, a : a + 1],
-                )
+        for a in range(2):
+            for r in range(2):
+                nc.scalar.activation(gated[a][r][:], turned[a][r], COPY, scale=g2_cols[r][:, a : a + 1])
         out_blocks = out.rearrange("(n p) t -> p n t", p=P)
         for a in range(2):
             turn_sums(gated[a], range(2), banks[4 + a])
@@ -386,7 +384,8 @@ def tile_moe_ser_relu_kernel(
             gated_gather(0, r, 0, TV)
         gated_gather(1, 0, 0, TV)
         finish(0)
-        for n, lo, hi in OUT_RUNS[1:]:
+        for i, (n, lo, hi) in enumerate(OUT_RUNS[1:]):
             gated_gather(n, 1, lo, hi)
-        finish(1)
-        finish(2)
+            if i > 0:
+                finish(i)
+        finish(len(OUT_RUNS) - 1)

@@ -186,7 +186,6 @@ def tile_moe_ser_relu_kernel(
         multiply(low_rows, banks[0], 1)
         relu_out(low_rows, banks[0])
         multiply(third_rows, banks[1], 1)
-        relu_out(third_rows, banks[1])
         late = [(3, fifth, sixth), (0, sixth, mid)]
         gather_words(0, sixth, S)
         multiply(late, banks[2], 0)
@@ -197,6 +196,7 @@ def tile_moe_ser_relu_kernel(
         multiply([(0, mid, S)], banks[4], 1)
         relu_out([(0, mid, S)], banks[4])
         nc.vector.tensor_scalar_max(h[0][:, sixth:mid], banks[2][:, C : C + P], 0.0)
+        nc.vector.tensor_scalar_max(h[2][:, fifth:sixth], banks[1][:, :C], 0.0)
         nc.vector.tensor_scalar_max(h[3][:, fifth:sixth], banks[2][:, :C], 0.0)
         for s in range(2):
             for j in range(1, 4):
@@ -348,7 +348,7 @@ def tile_moe_ser_relu_kernel(
 
         part = [[sb.tile([P, TV], F32, name=f"part{n}_{r}", align_bytes=64) for r in range(2)] for n in range(2)]
         res = [sb.tile([P, TV], F32, name=f"res{n}", align_bytes=64) for n in range(2)]
-        bare = [[sb.tile([P, TS], F32, name=f"bare{n}_{r}", align_bytes=64) for r in range(2)] for n in range(2)]
+        bare = [[sb.tile([P, TS + P], F32, name=f"bare{n}_{r}", align_bytes=64) for r in range(2)] for n in range(2)]
         gated = [[sb.tile([P, N], F32, name=f"gated{a}_{r}", align_bytes=64) for r in range(2)] for a in range(2)]
         s_res = [sb.tile([P, 2, P], F32, name=f"s_res{a}", align_bytes=64) for a in range(2)]
 
@@ -364,6 +364,8 @@ def tile_moe_ser_relu_kernel(
         for a in range(2):
             for r in range(2):
                 nc.scalar.activation(gated[a][r][:], turned[a][r], COPY, scale=g2_cols[r][:, a : a + 1])
+        handed = bare[0][1][:, P:]
+        nc.scalar.activation(handed, y[1][:].indirect(entries(pos_2[0], C, TV)), COPY)
         out_blocks = out.rearrange("(n p) t -> p n t", p=P)
         for a in range(2):
             turn_sums(gated[a], range(2), banks[4 + a])
@@ -382,10 +384,10 @@ def tile_moe_ser_relu_kernel(
 
         for r in range(2):
             gated_gather(0, r, 0, TV)
-        gated_gather(1, 0, 0, TV)
+        gated_gather(1, 0, 0, C)
         finish(0)
-        for i, (n, lo, hi) in enumerate(OUT_RUNS[1:]):
-            gated_gather(n, 1, lo, hi)
-            if i > 0:
-                finish(i)
-        finish(len(OUT_RUNS) - 1)
+        gated_gather(1, 1, 0, C)
+        gated_gather(1, 1, C, TV)
+        nc.vector.tensor_tensor(part[1][0][:, C:], handed, g2[:, 0, C:], MULT)
+        for i in range(1, len(OUT_RUNS)):
+            finish(i)

from contextlib import ExitStack

import concourse.mybir as mybir
from concourse.masks import make_identity

K, T, E, C, H, N = 1024, 768, 6, 256, 512, 256
S = E * C
P = 128
FLOPS = 2 * S * (K * H + H * N)

F32 = mybir.dt.float32
BF16 = mybir.dt.bfloat16
I32 = mybir.dt.int32
U32 = mybir.dt.uint32
U16 = mybir.dt.uint16
U8 = mybir.dt.uint8
FP8X4 = mybir.dt.float8_e4m3fn_x4
MULT = mybir.AluOpType.mult
ADD = mybir.AluOpType.add
RELU = mybir.ActivationFunctionType.Relu
COPY = mybir.ActivationFunctionType.Copy

HALF = S // 2
WIDE = 1024
TV = 512
TS = T - TV
RUNS = ((0, 512), (512, 1024), (1024, 1280), (1280, 1408), (1408, 1536))
OUT_RUNS = ((0, 0, 512), (1, 0, 256), (1, 256, 384), (1, 384, 512))


def entries(lst, first, last):
    return lst[:, first // 16 : last // 16]


def tile_moe_ser_relu_kernel(
    tc, x_words, x_scales, w1_words, w1_scales, w2_words, w2_scales, gate1, gate2,
    offs, pos1, pos2, offs2, pos3, pos4, out,
):
    nc = tc.nc
    with ExitStack() as ctx:
        sb = ctx.enter_context(tc.tile_pool(name="sb", bufs=1))
        ps = ctx.enter_context(tc.psum_pool(name="ps", bufs=1))
        banks = [ps.tile([P, 512], F32, name=f"bank{b}") for b in range(8)]

        def load_list(src, name):
            lst = sb.tile(list(src.shape), U16, name=name)
            nc.sync.dma_start(lst[:], src)
            return lst

        def load_gate_columns(gate, name, first):
            cols = [sb.tile([P, (T - first[r]) // P], F32, name=f"{name}_cols{r}") for r in range(2)]
            with nc.allow_non_contiguous_dma(reason="one gate value a token on the partitions"):
                for r in range(2):
                    nc.sync.dma_start(cols[r][:], gate[r, 0, first[r] :].rearrange("(a t) -> t a", t=P))
            return cols

        xs = sb.tile([P, WIDE], U8, name="xs", align_bytes=64)
        w1s = [sb.tile([P, E, H], U8, name=f"w1s{s}", align_bytes=64) for s in range(2)]
        w2s = sb.tile([P, E, N], U8, name="w2s", align_bytes=64)
        xw = sb.tile([P, 2 * T], U32, name="xw", align_bytes=64)
        nc.gpsimd.memset(xs[:].bitcast(I32), 0)
        for planes in w1s:
            nc.vector.memset(planes[:].bitcast(I32), 0)
        nc.vector.memset(w2s[:].bitcast(I32), 0)
        ident = sb.tile([P, P], F32, name="ident", align_bytes=64)
        make_identity(nc, ident[:])

        x_passes = x_words.rearrange("s p t d -> s p (t d)")
        nc.sync.dma_start(xw[:, :T].bitcast(I32), x_passes[0].bitcast(I32))
        offs_t = load_list(offs, "offs_t")
        for q in range(4):
            nc.sync.dma_start(
                xs[32 * q : 32 * q + 8, :T].bitcast(I32), x_scales[:, 4 * q : 4 * q + 4, :].bitcast(I32)
            )
        nc.sync.dma_start(xw[:, T:].bitcast(I32), x_passes[1].bitcast(I32))
        w1w = [sb.tile([P, 2, H], U32, name=f"w1w{e}", align_bytes=64) for e in range(E)]
        w1_passes = w1_words.rearrange("e s p i d -> p (e s) (i d)")
        w1_rows = w1_scales.rearrange("e s (q r) i -> s r q e i", r=4)

        def load_w1_words(e):
            nc.sync.dma_start(w1w[e][:].bitcast(I32), w1_passes[:, 2 * e : 2 * e + 2, :].bitcast(I32))

        def load_w1_scales(s):
            for r in range(4):
                nc.sync.dma_start(w1s[s][4 * s + r : P : 32].bitcast(I32), w1_rows[s, r].bitcast(I32))

        load_w1_words(0)
        for s in range(2):
            load_w1_scales(s)
        for e in range(1, E - 1):
            load_w1_words(e)
        w1_first = sb.tile([P, 2, P], U32, name="w1_first", align_bytes=64)
        nc.sync.dma_start(w1_first[:].bitcast(I32), w1_passes[:, 2 * E - 2 :, : 4 * P].bitcast(I32))
        pos_1 = [load_list(pos1, "pos1_t")]
        g1 = [sb.tile([P, TV], F32, name=f"g1_rows{r}") for r in range(2)]
        nc.sync.dma_start(g1[0][:], gate1[0, :, :TV])
        nc.sync.dma_start(w1w[E - 1][:, :, P:].bitcast(I32), w1_passes[:, 2 * E - 2 :, 4 * P :].bitcast(I32))
        pos_1.append(load_list(pos2, "pos2_t"))
        nc.sync.dma_start(g1[1][:], gate1[1, :, :TV])
        g1_cols = load_gate_columns(gate1, "g1", (TV, TV))
        offs2_t = load_list(offs2, "offs2_t")
        w2w = sb.tile([P, E, N], U32, name="w2w", align_bytes=64)
        nc.sync.dma_start(w2w[:].bitcast(I32), w2_words.rearrange("e s p n d -> p (e s) (n d)").bitcast(I32))
        w2_rows = w2_scales.rearrange("e s (q r) n -> r q (e s) n", r=4)
        for r in range(4):
            nc.sync.dma_start(w2s[r:P:32, :, :].bitcast(I32), w2_rows[r].bitcast(I32))
        pos_2 = [load_list(pos3, "pos3_t"), load_list(pos4, "pos4_t")]
        g2 = sb.tile([P, 2, TV], F32, name="g2_rows")
        nc.sync.dma_start(g2[:], gate2[:, :, :TV].rearrange("r p t -> p r t"))
        g2_cols = load_gate_columns(gate2, "g2", (TV, TV))

        xg = sb.tile([P, 8 * C], U32, name="xg", align_bytes=64)
        xgs = sb.tile([P, 5 * C], U8, name="xgs", align_bytes=64)
        h = [sb.tile([P, S], F32, name=f"h{j}", align_bytes=64) for j in range(4)]
        word_place = ((0, 1, 5, 6, 3, 4), (2, 3, 4, 7, 5, 6))
        scale_place = (2, 3, 4, 0, 1, 2)

        def words_at(s, lo, hi):
            start = word_place[s][lo // C] * C + lo % C
            return xg[:, start : start + hi - lo]

        def scales_at(s, lo, hi):
            start = scale_place[lo // C] * C + lo % C
            return xgs[4 * s : P, start : start + hi - lo]

        def gather_words(s, lo, hi):
            window = xw[:, T:] if s == 1 else (xw[:, :WIDE] if lo == 2 * C else xw[:, :T])
            nc.vector.tensor_copy(words_at(s, lo, hi), window.indirect(entries(offs_t, lo, hi)))

        def gather_scales(lo, hi):
            nc.vector.tensor_copy(scales_at(0, lo, hi), xs[:].indirect(entries(offs_t, lo, hi)))

        def multiply(pieces, bank, s):
            col = 0
            for n, (j, lo, hi) in enumerate(pieces):
                e = lo // C
                words = w1_first if (e == E - 1 and j == 0) else w1w[e]
                nc.tensor.matmul_mx(
                    bank[:, col : col + hi - lo],
                    lhsT=words[:, s, j * P : (j + 1) * P].bitcast(FP8X4),
                    lhsT_scale=w1s[s][4 * s : P, e, j * P : (j + 1) * P],
                    rhs=words_at(s, lo, hi).bitcast(FP8X4),
                    rhs_scale=scales_at(s, lo, hi),
                    start=(s == 0 and n == 0),
                    stop=(s == 1 and n == len(pieces) - 1),
                )
                col = col + hi - lo

        def relu_out(pieces, bank):
            col = 0
            for j, lo, hi in pieces:
                nc.scalar.activation(h[j][:, lo:hi], bank[:, col : col + hi - lo], RELU)
                col = col + hi - lo

        def first_layer(pieces, bank):
            for s in range(2):
                multiply(pieces, bank, s)
            relu_out(pieces, bank)

        def one_expert(e, first_bank):
            halves = [[(j, e * C, (e + 1) * C) for j in (2 * jj, 2 * jj + 1)] for jj in range(2)]
            for s in range(2):
                for jj in range(2):
                    multiply(halves[jj], banks[first_bank + jj], s)
            for jj in range(2):
                relu_out(halves[jj], banks[first_bank + jj])

        gather_words(0, 0, 2 * C)
        gather_scales(0, HALF)
        gather_words(1, 0, C)
        one_expert(0, 0)
        gather_words(1, C, 3 * C)
        one_expert(1, 2)
        gather_words(0, 2 * C, 4 * C)
        one_expert(2, 4)
        gather_words(1, 3 * C, 4 * C)
        gather_scales(HALF, S)
        one_expert(3, 6)
        fifth, sixth, mid = 4 * C, 5 * C, 5 * C + P
        low_rows = [(0, fifth, sixth), (1, fifth, sixth)]
        third_rows = [(2, fifth, sixth)]
        gather_words(0, fifth, sixth)
        multiply(low_rows, banks[0], 0)
        multiply(third_rows, banks[1], 0)
        gather_words(1, fifth, sixth)
        multiply(low_rows, banks[0], 1)
        relu_out(low_rows, banks[0])
        multiply(third_rows, banks[1], 1)
        late = [(3, fifth, sixth), (0, sixth, mid)]
        gather_words(0, sixth, S)
        multiply(late, banks[2], 0)
        multiply([(0, mid, S)], banks[4], 0)
        gather_words(1, sixth, mid)
        multiply(late, banks[2], 1)
        gather_words(1, mid, S)
        multiply([(0, mid, S)], banks[4], 1)
        relu_out([(0, mid, S)], banks[4])
        nc.vector.tensor_scalar_max(h[0][:, sixth:mid], banks[2][:, C : C + P], 0.0)
        nc.vector.tensor_scalar_max(h[2][:, fifth:sixth], banks[1][:, :C], 0.0)
        nc.vector.tensor_scalar_max(h[3][:, fifth:sixth], banks[2][:, :C], 0.0)
        for s in range(2):
            for j in range(1, 4):
                multiply([(j, sixth, S)], banks[4 + j], s)
        for j in range(1, 4):
            relu_out([(j, sixth, S)], banks[4 + j])

        later = [banks[b] for b in (0, 1, 5, 6, 4, 3, 2, 7)]
        prod = [[sb.tile([P, TV], F32, name=f"prod{j}_{r}", align_bytes=64) for r in range(2)] for j in range(4)]
        plain = [[sb.tile([P, TS], F32, name=f"plain{j}_{r}", align_bytes=64) for r in range(2)] for j in range(4)]
        c_flat = sb.tile([P, TV // P * H], BF16, name="c_flat", align_bytes=64)
        s_rows = [[sb.tile([P, P, 2], BF16, name=f"s_rows{a}_{u}", align_bytes=64) for u in range(2)] for a in range(2)]
        scaled = [sb.tile([P, 2, P, 2], F32, name=f"scaled{a}", align_bytes=64) for a in range(2)]
        c_pairs = sb.tile([P, 2 * T], U32, name="c_pairs", align_bytes=64)

        def turn_sums(pair, tiles, bank):
            for r in range(2):
                for n, t in enumerate(tiles):
                    nc.tensor.matmul(
                        bank[:, n * P : (n + 1) * P], lhsT=pair[r][:, t * P : (t + 1) * P], rhs=ident[:],
                        is_transpose=True, start=(r == 0 and n == 0), stop=(r == 1 and n == len(tiles) - 1),
                    )

        def vector_share(j, tiles, bank):
            lo, hi = tiles[0] * P, (tiles[-1] + 1) * P
            for r in range(2):
                nc.vector.tensor_tensor(
                    prod[j][r][:, lo:hi], h[j][:].indirect(entries(pos_1[r], lo, hi)), g1[r][:, lo:hi], MULT
                )
            turn_sums(prod[j], tiles, bank)

        def round_sums(j, tiles, bank):
            nc.scalar.copy(
                c_flat[:, tiles[0] * H : (tiles[-1] + 1) * H].rearrange("t (a u j m) -> t j u a m", u=2, j=4, m=64)[:, j]
                .rearrange("t u a (p v) -> t u a p v", v=2),
                bank[:, : len(tiles) * P].rearrange("t (a p u v) -> t u a p v", p=32, u=2, v=2),
            )

        def scalar_share(j, r):
            nc.scalar.activation(plain[j][r][:], h[j][:].indirect(entries(pos_1[r], TV, T)), COPY)
            for a in range(2):
                nc.tensor.transpose(
                    later[2 * (1 - r) + a][:, j * P : (j + 1) * P], plain[j][r][:, a * P : (a + 1) * P], ident[:]
                )

        def pairs_of(t, u):
            if t < TV // P:
                return c_flat[:, t * H + u * 2 * P : t * H + (u + 1) * 2 * P].bitcast(F32)
            return s_rows[t - TV // P][u][:].rearrange("t p v -> t (p v)").bitcast(F32)

        def turn_back(u, tiles, bank):
            for n, t in enumerate(tiles):
                nc.tensor.transpose(bank[:, n * P : (n + 1) * P], pairs_of(t, u), ident[:])

        def keep_pairs(u, tiles, bank, copy):
            first = u * T + tiles[0] * P
            copy(c_pairs[:, first : first + len(tiles) * P].bitcast(F32), bank[:, : len(tiles) * P])

        four = range(4)
        vector_share(0, four, later[7])
        vector_share(1, four, later[4])
        for j in four:
            scalar_share(j, 1)
        for a in range(2):
            nc.scalar.activation(
                scaled[a][:], later[a][:].rearrange("t (p u v) -> t u p v", u=2, v=2), COPY,
                scale=g1_cols[1][:, a : a + 1],
            )
        for j in four:
            scalar_share(j, 0)
        vector_share(2, four, later[5])
        round_sums(0, four, later[7])
        round_sums(1, four, later[4])
        round_sums(2, four, later[5])
        vector_share(3, range(0, 2), later[7])
        round_sums(3, range(0, 2), later[7])
        turn_back(0, range(0, 2), later[0])
        vector_share(3, range(2, 3), later[4])
        round_sums(3, range(2, 3), later[4])
        vector_share(3, range(3, 4), later[7])
        round_sums(3, range(3, 4), later[7])
        keep_pairs(0, range(0, 2), later[0], nc.scalar.copy)
        for u in range(2):
            for a in range(2):
                nc.vector.scalar_tensor_tensor(
                    s_rows[a][u][:], later[2 + a][:].rearrange("t (p u v) -> t u p v", u=2, v=2)[:, u],
                    g1_cols[0][:, a : a + 1], scaled[a][:, u], MULT, ADD,
                )
        turn_back(0, range(4, 6), later[4])
        keep_pairs(0, range(4, 6), later[4], nc.vector.tensor_copy)
        turn_back(0, range(2, 4), later[1])
        keep_pairs(0, range(2, 4), later[1], nc.scalar.copy)
        turn_back(1, four, later[7])
        keep_pairs(1, four, later[7], nc.scalar.copy)
        turn_back(1, range(4, 6), later[4])
        keep_pairs(1, range(4, 6), later[4], nc.scalar.copy)

        ring = [sb.tile([P, 2 * 512], U32, name=f"ring{b}", align_bytes=64) for b in range(4)]
        spare = [sb.tile([P, 2 * P], U32, name=f"spare{b}", align_bytes=64) for b in range(2)]
        apart = [ring[0][:], ring[2][:], ring[1][:], ring[3][:, : 2 * P], ring[3][:, 2 * P :]]
        woven = [ring[1], ring[3], ring[0], spare[0], spare[1]]
        cq = sb.tile([P, S], U32, name="cq", align_bytes=64)
        cqs = sb.tile([P, S], U8, name="cqs", align_bytes=64)
        y = [sb.tile([P, S], F32, name=f"y{n}", align_bytes=64) for n in range(2)]

        def gather_pairs(run):
            lo, hi = RUNS[run]
            width = hi - lo
            for u in range(2):
                window = c_pairs[:, T:] if u == 1 else (c_pairs[:, :T] if run == 0 else c_pairs[:])
                nc.vector.tensor_copy(
                    apart[run][:, u * width : (u + 1) * width], window.indirect(entries(offs2_t, lo, hi))
                )
            nc.scalar.copy(
                woven[run][:, : 2 * width].rearrange("p (m u) -> p m u", u=2),
                apart[run][:, : 2 * width].rearrange("p (u m) -> p m u", u=2),
            )

        def second_layer(run):
            lo, hi = RUNS[run]
            nc.vector.quantize_mx(
                cq[:, lo:hi].bitcast(FP8X4), cqs[:, lo:hi], woven[run][:, : 2 * (hi - lo)].bitcast(BF16)
            )
            for n in range(2):
                acc = banks[(2 * run + n) % 8]
                for first in range(lo, hi, C):
                    last = min(first + C, hi)
                    nc.tensor.matmul_mx(
                        acc[:, first - lo : last - lo],
                        lhsT=w2w[:, first // C, n * P : (n + 1) * P].bitcast(FP8X4),
                        lhsT_scale=w2s[:, first // C, n * P : (n + 1) * P],
                        rhs=cq[:, first:last].bitcast(FP8X4),
                        rhs_scale=cqs[:, first:last],
                        start=True,
                        stop=True,
                    )
                copy = nc.vector.tensor_copy if (run == 3 or (run, n) == (4, 0)) else nc.scalar.copy
                copy(y[n][:, lo:hi], acc[:, : hi - lo])

        gather_pairs(0)
        gather_pairs(1)
        second_layer(0)
        gather_pairs(2)
        second_layer(1)
        gather_pairs(3)
        gather_pairs(4)
        for run in (2, 3, 4):
            second_layer(run)

        part = [[sb.tile([P, TV], F32, name=f"part{n}_{r}", align_bytes=64) for r in range(2)] for n in range(2)]
        res = [sb.tile([P, TV], F32, name=f"res{n}", align_bytes=64) for n in range(2)]
        bare = [[sb.tile([P, TS + P], F32, name=f"bare{n}_{r}", align_bytes=64) for r in range(2)] for n in range(2)]
        gated = [[sb.tile([P, N], F32, name=f"gated{a}_{r}", align_bytes=64) for r in range(2)] for a in range(2)]
        s_res = [sb.tile([P, 2, P], F32, name=f"s_res{a}", align_bytes=64) for a in range(2)]

        turned = [[banks[2][:, a * N : (a + 1) * N], banks[3 + 3 * a][:, :N]] for a in range(2)]
        for r, tiles in ((0, range(2)), (1, range(1)), (1, range(1, 2))):
            lo, hi = tiles[0] * P, (tiles[-1] + 1) * P
            for n in (1, 0):
                nc.scalar.activation(bare[n][r][:, lo:hi], y[n][:].indirect(entries(pos_2[r], TV + lo, TV + hi)), COPY)
                for a in tiles:
                    nc.tensor.transpose(
                        turned[a][r][:, n * P : (n + 1) * P], bare[n][r][:, a * P : (a + 1) * P], ident[:]
                    )
        for a in range(2):
            for r in range(2):
                nc.scalar.activation(gated[a][r][:], turned[a][r], COPY, scale=g2_cols[r][:, a : a + 1])
        handed = bare[0][1][:, P:]
        nc.scalar.activation(handed, y[1][:].indirect(entries(pos_2[0], C, TV)), COPY)
        out_blocks = out.rearrange("(n p) t -> p n t", p=P)
        for a in range(2):
            turn_sums(gated[a], range(2), banks[4 + a])
            nc.scalar.copy(s_res[a][:].rearrange("p n t -> p (n t)"), banks[4 + a][:, :N])
            nc.scalar.dma_start(out_blocks[:, :, TV + a * P : TV + (a + 1) * P], s_res[a][:])

        def finish(i):
            n, lo, hi = OUT_RUNS[i]
            nc.vector.tensor_add(res[n][:, lo:hi], part[n][0][:, lo:hi], part[n][1][:, lo:hi])
            nc.sync.dma_start(out[n * P : (n + 1) * P, lo:hi], res[n][:, lo:hi])

        def gated_gather(n, r, lo, hi):
            nc.vector.tensor_tensor(
                part[n][r][:, lo:hi], y[n][:].indirect(entries(pos_2[r], lo, hi)), g2[:, r, lo:hi], MULT
            )

        for r in range(2):
            gated_gather(0, r, 0, TV)
        gated_gather(1, 0, 0, C)
        finish(0)
        gated_gather(1, 1, 0, C)
        gated_gather(1, 1, C, TV)
        nc.vector.tensor_tensor(part[1][0][:, C:], handed, g2[:, 0, C:], MULT)
        for i in range(1, len(OUT_RUNS)):
            finish(i)
